import numpy as np, ml_dtypes
CORES = [9,25,41,57]
N = 4
BF = ml_dtypes.bfloat16
def gentries(a):
    return np.ascontiguousarray(a.reshape(8, 16, -1).transpose(0, 2, 1)).reshape(8, -1)
def gtable(e):
    e = np.asarray(e); return np.ascontiguousarray(e.reshape(8, -1, 16).transpose(0, 2, 1)).reshape(128, -1).astype(np.int32)
W, NW, P, RO, F = 4096, 256, 16, 4, 1
S = W // NW
def parts(rng):
    x = rng.integers(0, 16, (N, 8, 16, W)); l = rng.integers(0, W, (N, 8, NW, P))
    n = np.where(rng.random((N, 8, NW)) < 0.12, rng.integers(0, P + 1, (N, 8, NW)), rng.integers(P // 2, P + 1, (N, 8, NW)))
    return x, l, n, rng.integers(0, 256, (N, 8, 16)), rng.integers(68, 100, (N, 8))
def pack(x, l, n, w, t):
    return {"xv": np.ascontiguousarray(x.reshape(N, 128, W)).astype(np.float32).astype(BF), "wl": np.stack([gtable(a.reshape(8, NW * P)) for a in l]),
            "wn": np.ascontiguousarray(n).astype(np.int32), "wt": np.ascontiguousarray(w.reshape(N, 128, 1)).astype(np.int32), "th": np.ascontiguousarray(t.reshape(N, 8, 1)).astype(np.int32)}
def setup_inputs(rng):
    return pack(*parts(rng))
def setup_inputs_alike(rng):
    x, l, n, w, t = parts(rng)
    l[:, ::2] = rng.choice(np.array([0, W - 1, W // 2, 3]), (N, 4, NW, P))
    l[:, 1] = l[:, 1, :, :1]; x[:, 3] = x[:, 3, :, :1]; w[:, 5] = 0; n[:, 6] = P; t[:, 7] = 0
    return pack(x, l, n, w, t)
def setup_inputs_corners(rng):
    x, l, n, w, t = parts(rng); k = np.arange(P)
    x = rng.integers(0, 4, (N, 8, 16, W)) + 12 * (np.arange(W) & 1); t = rng.integers(48, 144, (N, 8)); t[:, 0] = 48; t[:, 7] = 143
    w = np.where(rng.random((N, 8, 1)) < 0.3, 255 * rng.integers(0, 2, (N, 8, 1)), w)
    n = rng.choice(np.array([0, 1, 2, P - 1, P, P, P, P]), (N, 8, NW)); m = np.minimum(n, rng.choice(np.array([1, 2, P // 2, P // 2 + 1, P - 1, P]), (N, 8, NW)))
    pick = rng.random((8, NW)) < 0.4; a = rng.integers(P // 2, P + 1, (8, NW)); a[:, 0] = P // 2 + 1; a[:, NW - 1] = P; pick[:, 0] = True; pick[:, NW - 1] = True
    for q in range(0, N - 1, 2):
        m[q] = np.where(pick, a, m[q]); n[q] = np.where(pick, np.maximum(a, rng.integers(0, P + 1, (8, NW))), n[q])
        m[q + 1] = np.where(pick, P - a, m[q + 1]); n[q + 1] = np.where(pick, np.where(a == P, 0, np.maximum(P - a, rng.integers(1, P + 1, (8, NW)))), n[q + 1])
    m[0, 5] = P; n[0, 5] = P; m[1, 4] = 0; n[1, 4] = 0
    m[N - 2] = P; n[N - 2] = P; m[N - 1] = 0; n[N - 1] = 0
    for q in (0, 1):
        fr = np.where(pick, 0, m[q]); fr[5] = 0; fr = fr.reshape(-1); o = rng.permutation(8 * NW); b = fr[o]; cut = np.zeros_like(b)
        cut[o] = np.clip((int(np.sum(m[q])) - 256) % 512 - (np.add.accumulate(b) - b), 0, b)
        m[q] = m[q] - cut.reshape(8, NW); n[q] = np.where(m[q] == 0, 0, n[q])
    sc = np.where((k == 0) | (k >= n[..., None]), 2.0, rng.random((N, 8, NW, P)))
    brk = np.argsort(np.argsort(sc, axis=-1), axis=-1) < (m - 1)[..., None]
    cl = (rng.integers(0, 2, (N, 8, NW, 1)) + np.add.accumulate(brk.astype(np.int64), axis=-1)) & 1
    l = np.where(rng.random((N, 8, NW, P)) < 0.1, cl * (W - 1), 2 * rng.integers(0, W // 2, (N, 8, NW, P)) + cl)
    return pack(x, l, n, w, t)
def setup_inputs_ends(rng):
    kind = rng.integers(0, 3, (N, 8, 1, W)); k = np.arange(P); c = np.arange(1, P + 1)
    x = np.where(kind == 0, 0, np.where(kind == 1, 15, 15 * rng.integers(0, 2, (N, 8, 16, W))))
    for u, v in ((0, 15), ((240 * 255) & (W - 1), 0)):
        hh = ((u * u >> 5) + 37 * u + 611 * c) & (W - 1)
        for g in (0, 7): x[:, g][..., hh] = v
    x[..., 0] = 0; x[..., W - 1] = 15
    w = 255 * rng.integers(0, 2, (N, 8, 16)); w[:, 0] = 255; w[:, 7] = 255; w[:, 3, 0] = 0; w[:, 4] = 0
    t = 239 * rng.integers(0, 2, (N, 8)); t[:, 0] = 0; t[:, 1] = 239; t[:, 7] = 239
    kd = rng.integers(0, 4, (N, 8, NW, 1)); s = rng.integers(0, 2, (N, 8, NW, 1)); em = np.where(np.arange(N) == N - 1, 0.05, 0.25).reshape(N, 1, 1)
    kd[N - 1] = np.where(rng.random((8, NW, 1)) < 0.9, 1, kd[N - 1]); kd[:, :, 0] = 1; kd[:, 7, NW - 1] = 1; kd[:, 7, NW - 2] = 0; s[:, 7, NW - 2] = 1
    b = np.where(kd == 0, s, np.where(kd == 1, (k + s) & 1, rng.integers(0, 2, (N, 8, NW, P))))
    n = P * (rng.random((N, 8, NW)) > em).astype(np.int64); n[:, :, 0] = P; n[:, :, 1] = 0; n[:, :, NW - 2] = P; n[:, :, NW - 1] = P
    return pack(x, (W - 1) * b, n, w, t)
def setup_inputs_spread(rng):
    x, l, n, w, t = parts(rng)
    x = (rng.random((N, 8, 16, W)) * np.exp2(rng.integers(0, 5, (N, 8, 1, W)))).astype(np.int64)
    l = np.minimum((W * rng.random((N, 8, NW, P)) ** rng.choice(np.array([0.3, 1.0, 3.0]), (N, 8, 1, 1))).astype(np.int64), W - 1)
    n = rng.integers(0, P + 1, (N, 8, NW)); w = (256 * rng.random((N, 8, 16)) ** 2).astype(np.int64)
    t = np.exp2(7.9 * rng.random((N, 8))).astype(np.int64) - 1
    return pack(x, l, n, w, t)
def setup_inputs_ties(rng):
    x, l, n, w, t = parts(rng)
    lane = np.argsort(rng.random((N, 8, 16)), axis=-1); pm = np.argsort(rng.random((N, 8, W)), axis=-1)
    lev = np.zeros((N, 8, W), np.int64); np.put_along_axis(lev, pm, np.broadcast_to(np.arange(W) % 241, (N, 8, W)), 2)
    x = np.clip(lev[:, :, None, :] - 15 * lane[..., None], 0, 15)
    t = rng.choice(np.array([0, 1, 15, 16, 47, 80, 100]), (N, 8)); s = rng.integers(0, 241, (N, 8, NW))
    for k in range(P):
        l[..., k] = np.take_along_axis(pm, s + 241 * rng.integers(0, W // 241, (N, 8, NW)), 2)
        st = np.abs(t[:, :, None] + rng.integers(-1, 2, (N, 8, NW))); up = ((rng.random((N, 8, NW)) < 0.5) & (s + st <= 240)) | (s - st < 0)
        s = np.where(up, s + st, s - st)
    t[:, 7] = 239
    hl = 239 * ((np.arange(P) + rng.integers(0, 2, (N, NW, 1))) & 1) + rng.integers(0, 2, (N, NW, P)) + 241 * rng.integers(0, W // 241, (N, NW, P))
    l[:, 7] = np.take_along_axis(pm[:, 7], hl.reshape(N, NW * P), 1).reshape(N, NW, P)
    return pack(x, l, n, w, t)
def check_inputs(d):
    bad = []
    for k, lo, hi in (("xv", 0, 15), ("wl", 0, W - 1), ("wn", 0, P), ("wt", 0, 255), ("th", 0, 239)):
        v = np.asarray(d[k]).astype(np.float64)
        if not (np.min(v) >= lo and np.max(v) <= hi): bad.append("range of " + k)
        elif np.any(v != np.floor(v)): bad.append("whole numbers of " + k)
    return bad
def reference(xv, wl, wn, wt, th):
    x = xv.astype(np.int32).reshape(N, 8, 16, W); w = wt.astype(np.int32).reshape(N, 8, 16, 1, 1); lim = th.astype(np.int64).reshape(N, 8, 1, 1)
    l = np.stack([gentries(a) for a in wl]).astype(np.int64).reshape(N, 8, NW, P); n = wn.astype(np.int64)
    last = np.zeros((N, 1, 1, 1), np.int64); k = np.arange(P); M = W - 1
    for t in range(RO):
        if t > 0:
            l = np.roll(l, (1, 1), axis=(0, 1)); n = np.roll(n, (1, 1), axis=(0, 1))
        live = k < n[..., None]
        v = np.take_along_axis(x, l.reshape(N, 8, 1, NW * P), 3).reshape(N, 8, 16, NW, P)
        dist = np.add.reduce(np.abs(v[..., 1:] - v[..., :-1]), axis=2)
        start = live.copy(); start[..., 1:] &= dist > lim
        end = live.copy(); end[..., :-1] &= start[..., 1:] | ~live[..., 1:]
        num = np.add.accumulate(start.astype(np.int64), axis=-1) - 1; m = np.add.reduce(start.astype(np.int64), axis=-1)
        z = v.copy(); c = np.ones((N, 8, NW, P), np.int64); f = l.copy()
        for j in range(1, P):
            s = start[..., j]
            z[..., j] = np.where(s[:, :, None], v[..., j], np.maximum(z[..., j - 1], v[..., j]))
            c[..., j] = np.where(s, 1, c[..., j - 1] + 1); f[..., j] = np.where(s, l[..., j], f[..., j - 1])
        u = np.add.reduce(w * z, axis=2).astype(np.int64) & M
        h = ((u * u >> 5) + 37 * u + 611 * c) & M
        xh = np.take_along_axis(x, h.reshape(N, 8, 1, NW * P), 3).reshape(N, 8, 16, NW, P)
        dd = np.add.reduce(np.abs(xh - z), axis=2).astype(np.int64)
        y = np.zeros((N, 8, NW, 2 * P + 2), np.int64)
        np.put_along_axis(y, np.where(end, 2 * num, 2 * P), ((f * (2 * c + 1) >> 2) + last) & M, 3)
        np.put_along_axis(y, np.where(end, 2 * num + 1, 2 * P + 1), (h + dd * (2 * c + 1)) & M, 3)
        own = np.minimum(2 * m, P); over = np.roll(2 * m - own, 1, axis=0); oy = np.roll(y[..., P:2 * P], 1, axis=0)
        n = np.minimum(own + over, P); o = own[..., None]
        l = np.where(k < o, y[..., :P], np.where(k < n[..., None], np.take_along_axis(oy, np.clip(k - o, 0, P - 1), 3), 0))
        e = np.argmax(end, axis=-1)[..., None]; e5 = e[:, :, None]
        val = ((np.take_along_axis(z, e5, 4) + np.take_along_axis(xh, e5, 4)) >> 1)[..., 0]
        at = (S * np.arange(NW) + (np.take_along_axis(u, e, 3)[..., 0] & (S - 1)))[:, :, None]
        np.put_along_axis(x, at, np.where((m > 0)[:, :, None], val, np.take_along_axis(x, at, 3)), 3)
        last = np.add.reduce(m.reshape(N, 8 * NW), axis=1).reshape(N, 1, 1, 1) & 255
    return {"yx": np.add.reduce(x.reshape(N, 128, W // F, F), axis=3).astype(np.float32).astype(BF), "yl": np.stack([gtable(a.reshape(8, NW * P)) for a in l]).astype(np.float32), "yn": n.astype(np.float32)}

@@ -1,0 +1,573 @@
+from concourse.bass import DstId, RemoteDMATransfer
+from concourse.mybir import dt, AluOpType, AxisListType, ActivationFunctionType
+
+A = AluOpType
+F = ActivationFunctionType
+VISITS = 4
+SCRATCH = {
+    "X": ("sbuf", [128, 8192], "bfloat16"),
+    "ZZ": ("sbuf", [128, 4096], "bfloat16"), "XD": ("sbuf", [128, 4096], "bfloat16"),
+    "QB": ("sbuf", [128, 256], "bfloat16"),
+    "WL": ("sbuf", [128, 256], "int32"), "WN": ("sbuf", [8, 256], "int32"), "WT": ("sbuf", [128, 1], "int32"), "TH": ("sbuf", [8, 1], "int32"),
+    "WLF": ("sbuf", [128, 256], "float32"), "WNB": ("sbuf", [8, 256], "bfloat16"), "THB": ("sbuf", [8, 8], "bfloat16"),
+    "CI": ("sbuf", [128, 144], "int32"), "CG": ("sbuf", [128, 144], "int32"), "KI": ("sbuf", [128, 128], "int32"), "CS": ("sbuf", [128, 16], "int32"),
+    "PI": ("sbuf", [128, 4], "int32"), "PQ": ("sbuf", [128, 4], "int32"), "PR_": ("sbuf", [128, 4], "int32"),
+    "KF": ("sbuf", [128, 16], "float32"),
+    "IDB": ("sbuf", [128, 128], "bfloat16"), "NIB": ("sbuf", [128, 128], "bfloat16"), "IDF": ("sbuf", [128, 128], "float32"),
+    "BO": ("sbuf", [128, 128], "bfloat16"), "ZO": ("sbuf", [128, 144], "bfloat16"), "ZW": ("sbuf", [128, 144], "bfloat16"),
+    "SF": ("sbuf", [128, 8], "bfloat16"), "SGF": ("sbuf", [128, 16], "float32"), "SGB": ("sbuf", [128, 8], "bfloat16"), "SGT": ("sbuf", [8, 128], "bfloat16"),
+    "ON": ("sbuf", [128, 128], "bfloat16"), "NEG": ("sbuf", [128, 128], "bfloat16"), "RS": ("sbuf", [128, 128], "bfloat16"),
+    "BS": ("sbuf", [128, 16], "float32"),
+    "WI": ("sbuf", [128, 64], "int32"), "WF": ("sbuf", [128, 64], "float32"), "FE": ("sbuf", [128, 16], "uint16"), "TG": ("sbuf", [128, 16], "uint16"),
+    "ZF": ("sbuf", [128, 256], "bfloat16"), "SU": ("sbuf", [128, 256], "int32"), "SV": ("sbuf", [128, 256], "int32"),
+    "AI": ("sbuf", [128, 8], "int32"), "AF": ("sbuf", [128, 8], "float32"),
+    "YL": ("sbuf", [128, 256], "float32"), "YN": ("sbuf", [8, 256], "float32"),
+}
+for _h in (0, 1):
+    SCRATCH["V%d" % _h] = ("sbuf", [128, 2064], "bfloat16")
+    for _n in ("AD", "MK", "AE", "MO"):
+        SCRATCH["%s%d" % (_n, _h)] = ("sbuf", [128, 2048], "bfloat16")
+    SCRATCH["PD%d" % _h] = ("sbuf", [128, 2048], "float32")
+    SCRATCH["OF%d" % _h] = ("sbuf", [128, 128], "uint16")
+    SCRATCH["HU%d" % _h] = ("sbuf", [128, 128], "uint16")
+    SCRATCH["CT%d" % _h] = ("sbuf", [128, 144], "bfloat16")
+    SCRATCH["HB%d" % _h] = ("sbuf", [128, 128 * 16], "bfloat16")
+    SCRATCH["HF%d" % _h] = ("sbuf", [128, 128 * 6], "float32")
+    SCRATCH["HI%d" % _h] = ("sbuf", [128, 128 * 12], "int32")
+for _t in range(VISITS):
+    for _h in (0, 1):
+        SCRATCH["SN%d%d" % (_t, _h)] = ("sbuf", [128, 128], "float32")
+        SCRATCH["SM%d%d" % (_t, _h)] = ("sbuf", [128, 128], "bfloat16")
+        SCRATCH["RO%d%d" % (_t, _h)] = ("sbuf", [128, 64], "float32")
+        SCRATCH["RV%d%d" % (_t, _h)] = ("sbuf", [128, 64], "float32")
+        SCRATCH["RM%d%d" % (_t, _h)] = ("sbuf", [128, 128], "bfloat16")
+for _b in range(8):
+    SCRATCH["pb%d" % _b] = ("psum", [128, 512], "float32")
+ENGS = "VSTG"
+SEMAPHORES = ["e" + e for e in ENGS] + ["sent"] + ["rx%d%d" % (t, h) for t in range(VISITS) for h in (0, 1)] \
+    + ["rm%d%d" % (t, h) for t in range(VISITS) for h in (0, 1)] + ["dm%d" % i for i in range(12)]
+
+CYC, FIX, GAT, SCA, PE, HOP, OWN, NET = 1.0, 30.0, 1.6, 4.0, 0.5, 110.0, 40.0, 2800.0
+
+
+def R(b, c0, c1, step=1, p=128):
+    return (b, c0, c1, step, p)
+
+
+def _n(r):
+    return (r[2] - r[1] + r[3] - 1) // r[3]
+
+
+def _over(a, b):
+    if a[2] <= b[1] or b[2] <= a[1]:
+        return False
+    if a[3] == b[3] and a[3] > 1 and (a[1] - b[1]) % a[3]:
+        return False
+    return True
+
+
+def _wide(b):
+    return 4 if SCRATCH[b][2] in ("float32", "int32") else 2
+
+
+class Prog:
+    pass
+
+
+def build(g, T, topo, core):
+    ops = []
+    hist = {}
+    banks = {}
+    ndma = [0]
+
+    def ap(r):
+        if r is None or isinstance(r, (int, float)):
+            return r
+        if len(r) == 2:
+            w, o = r
+            if o is None:
+                return T[w][:]
+            return ap(w).indirect(ap(o))
+        b, c0, c1, st, p = r
+        full = SCRATCH[b][1][1]
+        if st == 1:
+            return T[b][0:p, c0:c1]
+        return T[b][0:p, c0:min(c1, full):st]
+
+    def regs(r):
+        if r is None or isinstance(r, (int, float)):
+            return []
+        if len(r) == 2:
+            return [] if r[1] is None else [r[0], r[1]]
+        return [r]
+
+    def add(eng, fn, reads, writes, cost, grp=None, dma=False, waits=(), after=(), lat=None):
+        i = len(ops)
+        deps = {}
+
+        def dep(j, hard):
+            if j != i:
+                deps[j] = deps.get(j, False) or hard
+        for r in reads:
+            for (q, j, w) in hist.get(r[0], ()):
+                if w and _over(q, r) and not (grp is not None and ops[j]["grp"] == grp):
+                    dep(j, True)
+        for r in writes:
+            for (q, j, w) in hist.get(r[0], ()):
+                if _over(q, r) and not (grp is not None and ops[j]["grp"] == grp):
+                    dep(j, w or ops[j]["eng"] != eng or ops[j]["dma"])
+        for b in set(r[0] for r in list(reads) + list(writes) if r[0][:2] == "pb"):
+            ph = banks.setdefault(b, [None, [], []])
+            if ph[0] != eng:
+                ph[2] = ph[1]
+                ph[0], ph[1] = eng, []
+            ph[1].append(i)
+            for j in ph[2]:
+                dep(j, True)
+        if grp is not None:
+            for j in range(i - 1, -1, -1):
+                if ops[j]["grp"] == grp:
+                    dep(j, False)
+                    break
+        for j in after:
+            dep(j, False)
+        for r in writes:
+            lst = hist.setdefault(r[0], [])
+            if r[3] == 1:
+                lst[:] = [e for e in lst if not (e[0][1] >= r[1] and e[0][2] <= r[2] and e[0][4] <= r[4])]
+            lst.append((r, i, True))
+        for r in reads:
+            hist.setdefault(r[0], []).append((r, i, False))
+        ops.append({"eng": eng, "fn": fn, "deps": deps, "cost": cost, "grp": grp, "dma": dma, "waits": waits, "lat": lat, "after": after})
+        return i
+
+    def vcost(out, ins, two=False):
+        n = _n(out)
+        w = max(_wide(r[0]) for q in [out] + list(ins) for r in regs(q)[:1])
+        ps = any(r[0][:2] == "pb" for q in ins for r in regs(q))
+        f = (1 if ps else 2) if two else (0.5 if w == 2 and not ps and out[0][:2] != "pb" else 1)
+        for q in ins:
+            if not isinstance(q, (int, float)) and q is not None and len(q) == 2:
+                f = max(f if two is False else 1, GAT)
+        return FIX + CYC * max(64, n * f)
+
+    def tt(out, a, b, op, **kw):
+        return add("V", lambda: g.vector.tensor_tensor(ap(out), ap(a), ap(b), op), regs(a) + regs(b), regs(out), vcost(out, [a, b], True), **kw)
+
+    def ts(out, a, s1, s2, op0, op1=None, **kw):
+        if op1 is None:
+            fn = lambda: g.vector.tensor_scalar(ap(out), ap(a), ap(s1), None, op0)
+        else:
+            fn = lambda: g.vector.tensor_scalar(ap(out), ap(a), ap(s1), ap(s2), op0, op1)
+        return add("V", fn, regs(a) + regs(s1) + regs(s2), regs(out), vcost(out, [a]), **kw)
+
+    def cp(out, a, **kw):
+        if len(out) == 2:
+            return add("V", lambda: g.vector.tensor_copy(ap(out), ap(a)), regs(a) + [out[1]], [out[0]], FIX + CYC * SCA * _n(a), **kw)
+        return add("V", lambda: g.vector.tensor_copy(ap(out), ap(a)), regs(a), regs(out), vcost(out, [a]), **kw)
+
+    def scan(out, d0, d1, op0, op1):
+        return add("V", lambda: g.vector.tensor_tensor_scan(ap(out), ap(d0), ap(d1), 0.0, op0, op1), regs(d0) + regs(d1), regs(out), vcost(out, [d0, d1]))
+
+    def ms(out, val):
+        return add("V", lambda: g.vector.memset(ap(out), val), [], regs(out), vcost(out, []))
+
+    def act(out, a, func, bias=0.0, scale=1.0):
+        n = _n(out) * (GAT if len(a) == 2 else 1)
+        return add("S", lambda: g.scalar.activation(ap(out), ap(a), func, bias=ap(bias), scale=scale), regs(a) + regs(bias), regs(out), FIX + 20 + CYC * max(64, n))
+
+    def mm(out, lhsT, rhs, start=True, stop=True, grp=None):
+        f = 4 if SCRATCH[lhsT[0]][2] == "float32" else 1
+        return add("T", lambda: g.tensor.matmul(ap(out), ap(lhsT), ap(rhs), start, stop), regs(lhsT) + regs(rhs), regs(out), 8 + PE * f * max(64, _n(rhs)), grp=grp)
+
+    def dma(q, out, a, cost=2500.0):
+        i = ndma[0]
+        ndma[0] += 1
+        eng = g.sync if q == "Q" else g.scalar
+        return add(q, lambda: eng.dma_start(ap(out), ap(a)), regs(a), regs(out), 100.0, dma="dm%d" % i, lat=cost)
+
+    def io(name, c0=None, c1=None):
+        return (name, None)
+
+    dma("Q", R("WL", 0, 256), ("wl", None))
+    dma("Q", R("X", 0, 4096), ("xv", None), 6000.0)
+    dma("S", R("TH", 0, 1, 1, 8), ("th", None))
+    dma("S", R("WN", 0, 256, 1, 8), ("wn", None))
+    dma("S", R("WT", 0, 1), ("wt", None))
+    add("G", lambda: g.iota(ap(R("CI", 0, 144)), [[1, 144]], 0, 0), [], [R("CI", 0, 144)], 400.0)
+    add("G", lambda: g.iota(ap(R("PI", 0, 1)), [[1, 1]], 0, 1), [], [R("PI", 0, 1)], 150.0)
+    PI = R("PI", 0, 1)
+    PF, PG, T15, K16, L16, WC, TB, PL = [R("KF", c, c + 1) for c in range(8)]
+    C128 = R("CI", 0, 128)
+    for h in (0, 1):
+        ms(R("V%d" % h, 0, 16), 0.0)
+        ms(R("CT%d" % h, 128, 144), 0.0)
+    ms(R("NEG", 0, 128), -1.0)
+    ms(R("ON", 0, 128), 1.0)
+    cp(PF, PI)
+    ts(R("PQ", 0, 1), PI, 4, None, A.logical_shift_right)
+    ts(R("PR_", 0, 1), PI, 15, None, A.bitwise_and)
+    cp(PG, R("PQ", 0, 1))
+    ts(T15, R("PQ", 0, 1), 16, 15, A.mult, A.add)
+    ts(K16, R("PR_", 0, 1), 16, 1, A.mult, A.add)
+    ts(L16, R("PR_", 0, 1), 16, None, A.mult)
+    ts(R("CG", 0, 144), R("CI", 0, 144), 4, None, A.logical_shift_right)
+    ts(R("SGT", 0, 128, 1, 8), R("CG", 0, 128, 1, 8), R("KF", 0, 1, 1, 8), None, A.is_equal)
+    ts(R("IDB", 0, 128), C128, PF, None, A.is_equal)
+    ts(R("NIB", 0, 128), C128, PF, -1, A.is_equal, A.mult)
+    ts(R("IDF", 0, 128), C128, PF, None, A.is_equal)
+    ts(R("BO", 0, 128), R("CG", 0, 128), PG, None, A.is_equal)
+    ts(R("ZO", 0, 144), R("CI", 0, 144), T15, None, A.is_equal)
+    ts(R("SF", 0, 8), R("CI", 0, 8), 16, PF, A.mult, A.is_equal)
+    ts(R("CS", 0, 16), R("CI", 0, 16), 7, None, A.bitwise_and)
+    ts(R("SGF", 0, 16), R("CS", 0, 16), PG, None, A.is_equal)
+    ts(R("SGB", 0, 8), R("CI", 0, 8), PG, None, A.is_equal)
+    ts(R("KI", 0, 128), C128, 15, None, A.bitwise_and)
+    ts(R("RS", 0, 128), R("KI", 0, 128), 0, None, A.is_gt)
+    ts(R("BS", 0, 16), R("CI", 0, 16), 256, L16, A.mult, A.add)
+    cp(R("THB", 0, 1, 1, 8), R("TH", 0, 1, 1, 8))
+    cp(R("WNB", 0, 256, 1, 8), R("WN", 0, 256, 1, 8))
+    cp(WC, R("WT", 0, 1))
+    ts(R("ZW", 0, 144), R("CI", 0, 144), T15, WC, A.is_equal, A.mult)
+    mm(R("pb3", 0, 1), R("SGT", 0, 128, 1, 8), R("THB", 0, 1, 1, 8))
+    ts(TB, R("pb3", 0, 1), 0.5, None, A.add)
+
+    def H(kind, h, s, c0=0, c1=128, step=1):
+        return R("%s%d" % (kind, h), 128 * s + c0, 128 * s + c1, step)
+
+    def hb(h, s, *a):
+        return H("HB", h, s, *a)
+
+    def hf(h, s, *a):
+        return H("HF", h, s, *a)
+
+    def hi(h, s, *a):
+        return H("HI", h, s, *a)
+    NL_, LV, EN, CU, CC, S1, G2, CD, CL, EL, E9, T1, OV, GL, UK = range(15)
+    NM, SNM, AA, PP, KC, FN = range(6)
+    JI, NMI, AG, AG2, P1, P1M, UI, U, Y, HH, Q2, Q3 = range(12)
+
+    def pA(h, r):
+        return R("pb%d" % (4 + 2 * h), 128 * r, 128 * r + 128)
+
+    def pB(h, r):
+        return R("pb%d" % (5 + 2 * h), 128 * r, 128 * r + 128)
+    rank = T.rank_of(core)
+    sends = [0]
+
+    def addr(d):
+        dst = T.cores[(rank + d) % 4]
+        rid, pid, _s = topo.addr(dst)
+        return dst, rid, pid
+
+    def start_words(h):
+        w = R("WL", 128 * h, 128 * h + 128)
+        cp(R("OF%d" % h, 0, 128), w)
+        cp(R("WLF", 128 * h, 128 * h + 128), w)
+        mm(pA(h, 0), R("WLF", 128 * h, 128 * h + 128), R("IDF", 0, 128))
+        act(hf(h, NM), pA(h, 0), F.Copy)
+        mm(pB(h, 0), R("WNB", 128 * h, 128 * h + 128, 1, 8), R("SGT", 0, 128, 1, 8))
+        tt(hb(h, LV), pB(h, 0), R("KI", 0, 128), A.is_gt)
+        ts(hb(h, NL_), hb(h, LV), -1, 1, A.mult, A.add)
+
+    def join(h, own, ov, waits, after):
+        tt(hi(h, JI, 0, 64), own, ov, A.add, waits=waits, after=after)
+        ts(hi(h, NMI, 0, 128, 2), hi(h, JI, 0, 64), 12, 4095, A.logical_shift_right, A.bitwise_and)
+        ts(hi(h, NMI, 1, 128, 2), hi(h, JI, 0, 64), 4095, None, A.bitwise_and)
+        cp(hf(h, NM), hi(h, NMI))
+        ts(hb(h, NL_, 0, 128, 2), hi(h, JI, 0, 64), 0, None, A.is_lt)
+        ts(hb(h, NL_, 1, 128, 2), hi(h, JI, 0, 64), 0, None, A.is_lt)
+        ts(hb(h, LV), hb(h, NL_), -1, 1, A.mult, A.add)
+
+    def offsets(h):
+        mm(pB(h, 0), hf(h, NM), R("IDF", 0, 128))
+        cp(R("OF%d" % h, 0, 128), pB(h, 0))
+
+    def front(t, h):
+        v, ad, mk = "V%d" % h, "AD%d" % h, "MK%d" % h
+        for c in range(4):
+            act(R(v, 16 + 512 * c, 528 + 512 * c), (R("X", 0, 4096), R("OF%d" % h, 32 * c, 32 * c + 32)), F.Copy)
+        for c in range(4):
+            b = R("pb%d" % c, 0, 512)
+            gr = ("df", t, h, c)
+            mm(b, R("IDB", 0, 128), R(v, 16 + 512 * c, 528 + 512 * c), True, False, gr)
+            mm(b, R("NIB", 0, 128), R(v, 15 + 512 * c, 527 + 512 * c), False, True, gr)
+            act(R(ad, 512 * c, 512 * c + 512), b, F.Abs)
+            mm(b, R("BO", 0, 128), R(ad, 512 * c, 512 * c + 512))
+            act(R(mk, 512 * c, 512 * c + 512), b, F.Sign, TB, -1.0)
+            act(R(mk, 512 * c, 512 * c + 512, 16), R("NEG", 0, 32), F.Copy)
+            scan(R("ZZ", 2048 * h + 512 * c, 2048 * h + 512 * c + 512), R(mk, 512 * c, 512 * c + 512), R(v, 16 + 512 * c, 528 + 512 * c), A.mult, A.max)
+        for k in range(16):
+            mm(R("pb%d" % (4 + 2 * h), k, 128, 16), R(mk, k, 2048, 16), R("SF", 0, 8))
+        ct = R("CT%d" % h, 0, 128)
+        tt(ct, pA(h, 0), hb(h, NL_), A.is_gt)
+        tt(hb(h, EN), hb(h, LV), R("CT%d" % h, 1, 129), A.subtract)
+        scan(hb(h, CU), R("RS", 0, 128), hb(h, EN), A.mult, A.add)
+        scan(hb(h, CC), ct, R("ON", 0, 128), A.mult, A.add)
+        tt(hb(h, CD), hb(h, CU), hb(h, EN), A.mult)
+        mm(pA(h, 1), hb(h, CC), R("IDB", 0, 128))
+        mm(pA(h, 2), hb(h, CD), R("IDB", 0, 128))
+        act(hf(h, KC), pA(h, 1), F.Copy, 0.0, 19552.0)
+        act(hb(h, GL), pA(h, 1), F.Copy, 1.0, 2.0)
+        act(hb(h, CL), pA(h, 2), F.Copy)
+        ts(hb(h, EL), hb(h, CL), 0.5, None, A.is_gt)
+        mm(pA(h, 0), R("BO", 0, 128), hb(h, EL))
+        sm = R("SM%d%d" % (t, h), 0, 128)
+        act(sm, pA(h, 0), F.Copy)
+        dst, rid, pid = addr(-1)
+        es = topo.engines(core, dst)
+        m = 0
+        for e in es[:8]:
+            m |= 1 << e
+        rm = "RM%d%d" % (t, h)
+        snd = add("G", lambda: g.remote_dma(out_ap=T[rm][:], in_ap=ap(sm), remote_sem=T.sem["rm%d%d" % (t, h)], local_sem=T.sem["sent"], pid=pid, routing_id=rid, dma_engine_mask=m),
+                  [sm], [], 1000.0, dma="sent", lat=NET)
+        sends[0] += 8
+        ts(hb(h, S1), ct, -1, 1, A.mult, A.add)
+        tt(hf(h, SNM), hf(h, NM), hb(h, S1), A.mult)
+        scan(hf(h, AA), ct, hf(h, SNM), A.mult, A.add)
+        ts(hb(h, G2), hb(h, CC), 2, 1, A.mult, A.add)
+        tt(hi(h, AG), hf(h, AA), hb(h, G2), A.mult)
+        if t == 0:
+            ts(hi(h, P1M), hi(h, AG), 2, 4095, A.logical_shift_right, A.bitwise_and)
+        else:
+            ts(hi(h, AG2), hi(h, AG), 2, None, A.logical_shift_right)
+            ts(hi(h, P1), hi(h, AG2), R("AF", t, t + 1), None, A.add)
+            ts(hi(h, P1M), hi(h, P1), 4095, None, A.bitwise_and)
+        ts(hf(h, PP), hi(h, P1M), 4096, 1, A.mult, A.add)
+        mm(pA(h, 3), hf(h, PP), R("IDF", 0, 128))
+        for s in range(8):
+            ts(R("MO%d" % h, 128 * s, 128 * s + 128), hb(h, CL), s + 1, None, A.is_equal)
+        ts(hb(h, E9), hb(h, CL), 9, 100, A.is_lt, A.mult)
+        tt(hb(h, T1), hb(h, CL), hb(h, E9), A.subtract)
+        tt(hb(h, OV), hb(h, T1), R(rm, 0, 128), A.add, waits=[("rm%d%d" % (t, h), 8)], after=[snd])
+        for s in range(8):
+            ts(R("MO%d" % h, 1024 + 128 * s, 1152 + 128 * s), hb(h, OV), s + 9, None, A.is_equal)
+
+    def middle(t, h):
+        gr = ("u", t, h)
+        for k in range(16):
+            mm(pB(h, 0), R("ZW", 15 - k, 143 - k), R("ZZ", 2048 * h + k, 2048 * h + 2048, 16), k == 0, k == 15, gr)
+        cp(hi(h, UI), pB(h, 0))
+        ts(hi(h, U), hi(h, UI), 4095, None, A.bitwise_and)
+        ts(pB(h, 1), hi(h, U), 1184, None, A.add)
+        tt(pB(h, 2), pB(h, 1), hi(h, U), A.mult)
+        tt(hi(h, Y), pB(h, 2), hf(h, KC), A.add)
+        ts(hi(h, HH), hi(h, Y), 5, 4095, A.logical_shift_right, A.bitwise_and)
+        cp(R("HU%d" % h, 0, 128), hi(h, HH))
+        for c in range(4):
+            a, b = 2048 * h + 512 * c, 2048 * h + 512 * c + 512
+            tt(R("XD", a, b), (R("X", 0, 4096), R("HU%d" % h, 32 * c, 32 * c + 32)), R("ZZ", a, b), A.subtract)
+            act(R("AE%d" % h, 512 * c, 512 * c + 512), R("XD", a, b), F.Abs)
+        ts(hi(h, UI), hi(h, U), 15, None, A.bitwise_and)
+        ts(hb(h, UK), hi(h, UI), K16, None, A.add)
+        tt(R("QB", 128 * h, 128 * h + 128), hb(h, UK), R("MO%d" % h, 0, 128), A.mult)
+
+    def write(t):
+        q = R("pb3", 0, 16)
+        gr = ("q", t)
+        for k in range(16):
+            mm(q, R("ZO", 15 - k, 143 - k), R("QB", k, 256, 16), k == 0, k == 15, gr)
+        qi, e, u, em = [R("WI", 16 * c, 16 * c + 16) for c in range(4)]
+        f1, f2 = R("WF", 0, 16), R("WF", 16, 32)
+        ts(qi, q, -1, None, A.add)
+        ts(e, qi, 4, 15, A.logical_shift_right, A.bitwise_and)
+        tt(f1, e, R("BS", 0, 16), A.add)
+        cp(R("FE", 0, 16), f1)
+        act(R("ZF", 0, 256), (R("ZZ", 0, 4096), R("FE", 0, 16)), F.Copy, 0.0, 2.0)
+        ts(u, qi, 15, None, A.bitwise_and)
+        ts(em, qi, 0, 4096, A.is_lt, A.mult)
+        tt(f2, u, R("BS", 0, 16), A.add)
+        f3 = R("WF", 32, 48)
+        tt(f3, f2, em, A.add)
+        cp(R("TG", 0, 16), f3)
+        tt(R("SU", 0, 256), (R("XD", 0, 4096), R("FE", 0, 16)), R("ZF", 0, 256), A.add)
+        ts(R("SV", 0, 256), R("SU", 0, 256), 1, None, A.arith_shift_right)
+        cp((R("X", 0, 8192), R("TG", 0, 16)), R("SV", 0, 256))
+        if t < VISITS - 1:
+            for h in (0, 1):
+                mm(R("pb2", 0, 128), R("ON", 0, 128), hb(h, EN), h == 0, h == 1, ("a", t))
+            add("V", lambda: g.vector.tensor_reduce(ap(R("AF", 4 + t, 5 + t)), ap(R("pb2", 0, 128)), axis=AxisListType.X, op=A.add), [R("pb2", 0, 128)], [R("AF", 4 + t, 5 + t)], FIX + 128)
+            cp(R("AI", 0, 1), R("AF", 4 + t, 5 + t))
+            ts(R("AI", 1, 2), R("AI", 0, 1), 255, None, A.bitwise_and)
+            cp(R("AF", t + 1, t + 2), R("AI", 1, 2))
+
+    def back(t, h):
+        gr = ("d", t, h)
+        for k in range(16):
+            mm(pB(h, 3), R("ZO", 15 - k, 143 - k), R("AE%d" % h, k, 2048, 16), k == 0, k == 15, gr)
+        tt(pB(h, 1), pB(h, 3), hb(h, GL), A.mult)
+        tt(hi(h, Q2), pB(h, 1), hi(h, HH), A.add)
+        ts(hi(h, Q3), hi(h, Q2), 4095, None, A.bitwise_and)
+        tt(pB(h, 2), pA(h, 3), hi(h, Q3), A.add)
+        last = t == VISITS - 1
+        sg = R("SGF", 0, 8) if last else R("SGF", 7, 15)
+        bank = "pb%d" % (4 + 2 * h)
+        for s in (list(range(8, 16)) + list(range(8)) if last else range(16)):
+            pr = R("PD%d" % h, 128 * s, 128 * s + 128)
+            tt(pr, pB(h, 2), R("MO%d" % h, 128 * s, 128 * s + 128), A.mult)
+            o = 64 * (s // 8)
+            mm(R(bank, o + s % 8, o + 64, 8), pr, sg)
+        sn = "SN%d%d" % (t, h)
+        act(R(sn, 0, 64), R(bank, 0, 64), F.Copy, -1.0)
+        act(R(sn, 64, 128), R(bank, 64, 128), F.Copy)
+        ro, rv, rx = "RO%d%d" % (t, h), "RV%d%d" % (t, h), "rx%d%d" % (t, h)
+        d1, r1, p1 = addr(1)
+        d2, r2, p2 = addr(2)
+        e1, e2 = topo.engines(core, d1), topo.engines(core, d2)
+        if last:
+            m = 0
+            for e in e1[:8]:
+                m |= 1 << e
+            sends[0] += 8
+            return add("G", lambda: g.remote_dma(out_ap=T[rv][:], in_ap=ap(R(sn, 64, 128)), remote_sem=T.sem[rx], local_sem=T.sem["sent"], pid=p1, routing_id=r1, dma_engine_mask=m),
+                       [R(sn, 64, 128)], [], 1000.0, dma="sent", lat=NET)
+        m1 = m2 = 0
+        for e in e1[:4]:
+            m1 |= 1 << e
+        for e in [e for e in e2 if e not in e1[:4]][:4]:
+            m2 |= 1 << e
+        sends[0] += 8
+
+        def fused():
+            return g.remote_dma_fused([
+                RemoteDMATransfer(dst_ids=[DstId(rid=r1, pnc=p1)], dma_engine_mask=m1, remote_sem=T.sem[rx], src=ap(R(sn, 0, 64)), dst=T[ro][:]),
+                RemoteDMATransfer(dst_ids=[DstId(rid=r2, pnc=p2)], dma_engine_mask=m2, remote_sem=T.sem[rx], src=ap(R(sn, 64, 128)), dst=T[rv][:]),
+            ], local_sem=T.sem["sent"])
+        return add("G", fused, [R(sn, 0, 128)], [], 1200.0, dma="sent", lat=NET)
+
+    arr = {}
+    for t in range(VISITS):
+        for h in (0, 1):
+            if t == 0:
+                start_words(h)
+            else:
+                q = "%d%d" % (t - 1, h)
+                join(h, R("RO" + q, 0, 64), R("RV" + q, 0, 64), [("rx" + q, 8)], [arr[h]])
+                offsets(h)
+        for h in (0, 1):
+            front(t, h)
+            middle(t, h)
+        write(t)
+        for h in (0, 1):
+            arr[h] = back(t, h)
+    dma("Q", ("yx", None), R("X", 0, 4096), 6000.0)
+    for h in (0, 1):
+        q = "%d%d" % (VISITS - 1, h)
+        join(h, R("SN" + q, 0, 64), R("RV" + q, 0, 64), [("rx" + q, 8)], [arr[h]])
+        ts(hf(h, SNM), hi(h, NMI), 1, None, A.add)
+        tt(hf(h, FN), hf(h, SNM), hb(h, LV), A.mult)
+        mm(pB(h, 0), hf(h, FN), R("IDF", 0, 128))
+        ts(R("YL", 128 * h, 128 * h + 128), pB(h, 0), -1, 0, A.add, A.max)
+        ts(hb(h, EL), pB(h, 0), 0.5, None, A.is_gt)
+        mm(R("pb%d" % (4 + 2 * h), 0, 128, 1, 8), R("SGB", 0, 8), hb(h, EL))
+        act(R("YN", 128 * h, 128 * h + 128, 1, 8), R("pb%d" % (4 + 2 * h), 0, 128, 1, 8), F.Copy)
+    dma("Q", ("yl", None), R("YL", 0, 256))
+    dma("Q", ("yn", None), R("YN", 0, 256, 1, 8))
+    return ops, sends[0]
+
+
+def schedule(ops):
+    n = len(ops)
+    succ = [[] for _ in range(n)]
+    npred = [0] * n
+
+    def lag(j, i, hard):
+        a, b = ops[j], ops[i]
+        if not hard and j not in b["after"]:
+            return None
+        if a["lat"] is not None:
+            return a["cost"] + a["lat"]
+        return a["cost"] + (OWN if a["eng"] == b["eng"] else HOP)
+    for i in range(n):
+        for j, hard in ops[i]["deps"].items():
+            succ[j].append((i, lag(j, i, hard)))
+            npred[i] += 1
+    prio = [0.0] * n
+    for i in range(n - 1, -1, -1):
+        best = ops[i]["cost"]
+        for (k, lg) in succ[i]:
+            best = max(best, prio[k] + (lg if lg is not None else 0.0))
+        prio[i] = best
+    ready = {e: [] for e in "VSTGQ"}
+    at = [0.0] * n
+    for i in range(n):
+        if npred[i] == 0:
+            ready[ops[i]["eng"]].append(i)
+    free = {e: 0.0 for e in ready}
+    order = []
+    start = [0.0] * n
+    while len(order) < n:
+        best = None
+        for e in ready:
+            if not ready[e]:
+                continue
+            t0 = min(max(free[e], at[i]) for i in ready[e])
+            if best is None or t0 < best[0]:
+                best = (t0, e)
+        t0, e = best
+        i = max((k for k in ready[e] if max(free[e], at[k]) <= t0 + 1e-9), key=lambda k: (prio[k], -k))
+        ready[e].remove(i)
+        start[i] = t0
+        order.append(i)
+        free[e] = t0 + ops[i]["cost"]
+        for (k, lg) in succ[i]:
+            at[k] = max(at[k], t0 + (lg if lg is not None else 0.0))
+            npred[k] -= 1
+            if npred[k] == 0:
+                ready[ops[k]["eng"]].append(k)
+    return order, start, free
+
+
+def rank_program(g, core, T, topo):
+    if T.rank_of(core) is None:
+        return
+    ops, nsent = build(g, T, topo, core)
+    order, start, free = schedule(ops)
+    queue = {"V": g.vector, "S": g.scalar, "T": g.tensor, "G": g, "Q": g.sync}
+    need = set()
+    for i in order:
+        for j, hard in ops[i]["deps"].items():
+            if hard and not ops[j]["dma"]:
+                need.add(j)
+    count = {e: 0 for e in queue}
+    mark = {}
+    know = {e: {} for e in queue}
+    snap = {}
+    for i in order:
+        o = ops[i]
+        e = o["eng"]
+        want = {}
+        for j, hard in o["deps"].items():
+            if not hard or ops[j]["dma"] == "sent":
+                continue
+            s, v = mark[j]
+            if know[e].get(s, 0) < v:
+                want.setdefault(s, []).append((v, j))
+        todo = sorted(((max(l)[0], s, max(l)[1]) for s, l in want.items()), key=lambda x: -start[x[2]])
+        for v, s, j in todo:
+            if know[e].get(s, 0) >= v:
+                continue
+            queue[e].wait_ge(T.sem[s], v)
+            know[e][s] = v
+            for s2, v2 in snap[j].items():
+                if know[e].get(s2, 0) < v2:
+                    know[e][s2] = v2
+        for (s, v) in o["waits"]:
+            queue[e].wait_ge(T.sem[s], v)
+        ins = o["fn"]()
+        snap[i] = dict(know[e])
+        if o["dma"] and o["dma"] != "sent":
+            ins.then_inc(T.sem[o["dma"]], 16)
+            mark[i] = (o["dma"], 16)
+        elif i in need:
+            count[e] += 1
+            ins.then_inc(T.sem["e" + e], 1)
+            mark[i] = ("e" + e, count[e])
+    for e in ENGS:
+        if count[e]:
+            g.wait_ge(T.sem["e" + e], count[e])
+    g.wait_ge(T.sem["sent"], nsent)
+    for o in ops:
+        if o["dma"] and o["dma"] != "sent":
+            g.wait_ge(T.sem[o["dma"]], 16)

@@ -7,7 +7,7 @@ VISITS = 4
 SCRATCH = {
     "X": ("sbuf", [128, 8192], "bfloat16"),
     "ZZ": ("sbuf", [128, 4096], "bfloat16"), "XD": ("sbuf", [128, 4096], "bfloat16"),
-    "QB": ("sbuf", [128, 256], "bfloat16"),
+    "QE": ("sbuf", [128, 256], "bfloat16"), "QU": ("sbuf", [128, 256], "bfloat16"), "M0": ("sbuf", [128, 256], "bfloat16"),
     "WL": ("sbuf", [128, 256], "int32"), "WN": ("sbuf", [8, 256], "int32"), "WT": ("sbuf", [128, 1], "int32"), "TH": ("sbuf", [8, 1], "int32"),
     "WLF": ("sbuf", [128, 256], "float32"), "WNB": ("sbuf", [8, 256], "bfloat16"), "THB": ("sbuf", [8, 8], "bfloat16"),
     "CI": ("sbuf", [128, 144], "int32"), "CG": ("sbuf", [128, 144], "int32"), "KI": ("sbuf", [128, 128], "int32"), "CS": ("sbuf", [128, 16], "int32"),
@@ -16,9 +16,9 @@ SCRATCH = {
     "IDB": ("sbuf", [128, 128], "bfloat16"), "NIB": ("sbuf", [128, 128], "bfloat16"), "IDF": ("sbuf", [128, 128], "float32"),
     "BO": ("sbuf", [128, 128], "bfloat16"), "ZO": ("sbuf", [128, 144], "bfloat16"), "ZW": ("sbuf", [128, 144], "bfloat16"),
     "SF": ("sbuf", [128, 8], "bfloat16"), "SGF": ("sbuf", [128, 16], "float32"), "SGB": ("sbuf", [128, 8], "bfloat16"), "SGT": ("sbuf", [8, 128], "bfloat16"),
-    "ON": ("sbuf", [128, 128], "bfloat16"), "NEG": ("sbuf", [128, 128], "bfloat16"), "RS": ("sbuf", [128, 128], "bfloat16"),
-    "BS": ("sbuf", [128, 16], "float32"),
-    "WI": ("sbuf", [128, 64], "int32"), "WF": ("sbuf", [128, 64], "float32"), "FE": ("sbuf", [128, 16], "uint16"), "TG": ("sbuf", [128, 16], "uint16"),
+    "ON": ("sbuf", [128, 128], "bfloat16"), "BIG": ("sbuf", [128, 32], "bfloat16"), "C4K": ("sbuf", [128, 16], "bfloat16"), "ZN": ("sbuf", [128, 144], "bfloat16"), "RS": ("sbuf", [128, 128], "bfloat16"),
+    "BS": ("sbuf", [128, 16], "bfloat16"),
+    "FE": ("sbuf", [128, 16], "uint16"), "TG": ("sbuf", [128, 16], "uint16"),
     "ZF": ("sbuf", [128, 256], "bfloat16"), "SU": ("sbuf", [128, 256], "int32"), "SV": ("sbuf", [128, 256], "int32"),
     "AI": ("sbuf", [128, 8], "int32"), "AF": ("sbuf", [128, 8], "float32"),
     "YL": ("sbuf", [128, 256], "float32"), "YN": ("sbuf", [8, 256], "float32"),
@@ -70,8 +70,7 @@ def _wide(b):
     return 4 if SCRATCH[b][2] in ("float32", "int32") else 2
 
 
-class Prog:
-    pass
+PLAN = {"gv": {0: (), 1: (0, 1, 2, 3)}, "xs": {0: (), 1: (2, 3)}, "bias": {}}
 
 
 def build(g, T, topo, core):
@@ -79,6 +78,8 @@ def build(g, T, topo, core):
     hist = {}
     banks = {}
     ndma = [0]
+    stage = [("load", 0, 0)]
+    blast = {}
 
     def ap(r):
         if r is None or isinstance(r, (int, float)):
@@ -124,6 +125,11 @@ def build(g, T, topo, core):
             ph[1].append(i)
             for j in ph[2]:
                 dep(j, True)
+        if eng == "T":
+            for b in set(r[0] for r in writes):
+                if b in blast and ops[blast[b]]["grp"] != grp:
+                    dep(blast[b], False)
+                blast[b] = i
         if grp is not None:
             for j in range(i - 1, -1, -1):
                 if ops[j]["grp"] == grp:
@@ -138,7 +144,7 @@ def build(g, T, topo, core):
             lst.append((r, i, True))
         for r in reads:
             hist.setdefault(r[0], []).append((r, i, False))
-        ops.append({"eng": eng, "fn": fn, "deps": deps, "cost": cost, "grp": grp, "dma": dma, "waits": waits, "lat": lat, "after": after})
+        ops.append({"stage": stage[0], "eng": eng, "fn": fn, "deps": deps, "cost": cost, "grp": grp, "dma": dma, "waits": waits, "lat": lat, "after": after})
         return i
 
     def vcost(out, ins, two=False):
@@ -176,9 +182,9 @@ def build(g, T, topo, core):
         n = _n(out) * (GAT if len(a) == 2 else 1)
         return add("S", lambda: g.scalar.activation(ap(out), ap(a), func, bias=ap(bias), scale=scale), regs(a) + regs(bias), regs(out), FIX + 20 + CYC * max(64, n))
 
-    def mm(out, lhsT, rhs, start=True, stop=True, grp=None):
+    def mm(out, lhsT, rhs, start=True, stop=True, grp=None, **kw):
         f = 4 if SCRATCH[lhsT[0]][2] == "float32" else 1
-        return add("T", lambda: g.tensor.matmul(ap(out), ap(lhsT), ap(rhs), start, stop), regs(lhsT) + regs(rhs), regs(out), 8 + PE * f * max(64, _n(rhs)), grp=grp)
+        return add("T", lambda: g.tensor.matmul(ap(out), ap(lhsT), ap(rhs), start, stop), regs(lhsT) + regs(rhs), regs(out), 8 + PE * f * max(64, _n(rhs)), grp=grp, **kw)
 
     def dma(q, out, a, cost=2500.0):
         i = ndma[0]
@@ -197,19 +203,20 @@ def build(g, T, topo, core):
     add("G", lambda: g.iota(ap(R("CI", 0, 144)), [[1, 144]], 0, 0), [], [R("CI", 0, 144)], 400.0)
     add("G", lambda: g.iota(ap(R("PI", 0, 1)), [[1, 1]], 0, 1), [], [R("PI", 0, 1)], 150.0)
     PI = R("PI", 0, 1)
-    PF, PG, T15, K16, L16, WC, TB, PL = [R("KF", c, c + 1) for c in range(8)]
+    PF, PG, T15, KC_, L16, WC, TB, PL = [R("KF", c, c + 1) for c in range(8)]
     C128 = R("CI", 0, 128)
     for h in (0, 1):
         ms(R("V%d" % h, 0, 16), 0.0)
         ms(R("CT%d" % h, 128, 144), 0.0)
-    ms(R("NEG", 0, 128), -1.0)
+    ms(R("BIG", 0, 32), 512.0)
+    ms(R("C4K", 0, 16), 4096.0)
     ms(R("ON", 0, 128), 1.0)
     cp(PF, PI)
     ts(R("PQ", 0, 1), PI, 4, None, A.logical_shift_right)
     ts(R("PR_", 0, 1), PI, 15, None, A.bitwise_and)
     cp(PG, R("PQ", 0, 1))
     ts(T15, R("PQ", 0, 1), 16, 15, A.mult, A.add)
-    ts(K16, R("PR_", 0, 1), 16, 1, A.mult, A.add)
+    cp(KC_, R("PR_", 0, 1))
     ts(L16, R("PR_", 0, 1), 16, None, A.mult)
     ts(R("CG", 0, 144), R("CI", 0, 144), 4, None, A.logical_shift_right)
     ts(R("SGT", 0, 128, 1, 8), R("CG", 0, 128, 1, 8), R("KF", 0, 1, 1, 8), None, A.is_equal)
@@ -218,6 +225,7 @@ def build(g, T, topo, core):
     ts(R("IDF", 0, 128), C128, PF, None, A.is_equal)
     ts(R("BO", 0, 128), R("CG", 0, 128), PG, None, A.is_equal)
     ts(R("ZO", 0, 144), R("CI", 0, 144), T15, None, A.is_equal)
+    ts(R("ZN", 0, 144), R("CI", 0, 144), T15, -4096, A.is_equal, A.mult)
     ts(R("SF", 0, 8), R("CI", 0, 8), 16, PF, A.mult, A.is_equal)
     ts(R("CS", 0, 16), R("CI", 0, 16), 7, None, A.bitwise_and)
     ts(R("SGF", 0, 16), R("CS", 0, 16), PG, None, A.is_equal)
@@ -267,8 +275,8 @@ def build(g, T, topo, core):
         mm(pA(h, 0), R("WLF", 128 * h, 128 * h + 128), R("IDF", 0, 128))
         act(hf(h, NM), pA(h, 0), F.Copy)
         mm(pB(h, 0), R("WNB", 128 * h, 128 * h + 128, 1, 8), R("SGT", 0, 128, 1, 8))
-        tt(hb(h, LV), pB(h, 0), R("KI", 0, 128), A.is_gt)
-        ts(hb(h, NL_), hb(h, LV), -1, 1, A.mult, A.add)
+        tt(pA(h, 1), pB(h, 0), R("KI", 0, 128), A.is_gt)
+        ts(hb(h, NL_), pA(h, 1), -1, 1, A.mult, A.add)
 
     def join(h, own, ov, waits, after):
         tt(hi(h, JI, 0, 64), own, ov, A.add, waits=waits, after=after)
@@ -277,40 +285,48 @@ def build(g, T, topo, core):
         cp(hf(h, NM), hi(h, NMI))
         ts(hb(h, NL_, 0, 128, 2), hi(h, JI, 0, 64), 0, None, A.is_lt)
         ts(hb(h, NL_, 1, 128, 2), hi(h, JI, 0, 64), 0, None, A.is_lt)
-        ts(hb(h, LV), hb(h, NL_), -1, 1, A.mult, A.add)
+        act(pA(h, 1), hb(h, NL_), F.Copy, 1.0, -1.0)
 
     def offsets(h):
         mm(pB(h, 0), hf(h, NM), R("IDF", 0, 128))
         cp(R("OF%d" % h, 0, 128), pB(h, 0))
 
+    def mask(h, s):
+        return R("M0", 128 * h, 128 * h + 128) if s == 0 else R("MO%d" % h, 128 * s, 128 * s + 128)
+
     def front(t, h):
+        stage[0] = ("front", t, h)
         v, ad, mk = "V%d" % h, "AD%d" % h, "MK%d" % h
         for c in range(4):
-            act(R(v, 16 + 512 * c, 528 + 512 * c), (R("X", 0, 4096), R("OF%d" % h, 32 * c, 32 * c + 32)), F.Copy)
+            o, i = R(v, 16 + 512 * c, 528 + 512 * c), (R("X", 0, 4096), R("OF%d" % h, 32 * c, 32 * c + 32))
+            if c in PLAN["gv"][h]:
+                cp(o, i)
+            else:
+                act(o, i, F.Copy)
         for c in range(4):
             b = R("pb%d" % c, 0, 512)
             gr = ("df", t, h, c)
             mm(b, R("IDB", 0, 128), R(v, 16 + 512 * c, 528 + 512 * c), True, False, gr)
-            mm(b, R("NIB", 0, 128), R(v, 15 + 512 * c, 527 + 512 * c), False, True, gr)
+            mm(b, R("NIB", 0, 128), R(v, 15 + 512 * c, 527 + 512 * c), False, False, gr)
+            mm(R("pb%d" % c, 0, 512, 16), R("IDB", 0, 128), R("BIG", 0, 32), False, True, gr)
             act(R(ad, 512 * c, 512 * c + 512), b, F.Abs)
             mm(b, R("BO", 0, 128), R(ad, 512 * c, 512 * c + 512))
             act(R(mk, 512 * c, 512 * c + 512), b, F.Sign, TB, -1.0)
-            act(R(mk, 512 * c, 512 * c + 512, 16), R("NEG", 0, 32), F.Copy)
             scan(R("ZZ", 2048 * h + 512 * c, 2048 * h + 512 * c + 512), R(mk, 512 * c, 512 * c + 512), R(v, 16 + 512 * c, 528 + 512 * c), A.mult, A.max)
         for k in range(16):
             mm(R("pb%d" % (4 + 2 * h), k, 128, 16), R(mk, k, 2048, 16), R("SF", 0, 8))
         ct = R("CT%d" % h, 0, 128)
         tt(ct, pA(h, 0), hb(h, NL_), A.is_gt)
-        tt(hb(h, EN), hb(h, LV), R("CT%d" % h, 1, 129), A.subtract)
-        scan(hb(h, CU), R("RS", 0, 128), hb(h, EN), A.mult, A.add)
+        tt(hb(h, EN), pA(h, 1), R("CT%d" % h, 1, 129), A.subtract)
+        scan(pA(h, 0), R("RS", 0, 128), hb(h, EN), A.mult, A.add)
         scan(hb(h, CC), ct, R("ON", 0, 128), A.mult, A.add)
-        tt(hb(h, CD), hb(h, CU), hb(h, EN), A.mult)
+        tt(hb(h, CD), pA(h, 0), hb(h, EN), A.mult)
         mm(pA(h, 1), hb(h, CC), R("IDB", 0, 128))
         mm(pA(h, 2), hb(h, CD), R("IDB", 0, 128))
         act(hf(h, KC), pA(h, 1), F.Copy, 0.0, 19552.0)
         act(hb(h, GL), pA(h, 1), F.Copy, 1.0, 2.0)
         act(hb(h, CL), pA(h, 2), F.Copy)
-        ts(hb(h, EL), hb(h, CL), 0.5, None, A.is_gt)
+        act(hb(h, EL), hb(h, CL), F.Sign)
         mm(pA(h, 0), R("BO", 0, 128), hb(h, EL))
         sm = R("SM%d%d" % (t, h), 0, 128)
         act(sm, pA(h, 0), F.Copy)
@@ -323,28 +339,19 @@ def build(g, T, topo, core):
         snd = add("G", lambda: g.remote_dma(out_ap=T[rm][:], in_ap=ap(sm), remote_sem=T.sem["rm%d%d" % (t, h)], local_sem=T.sem["sent"], pid=pid, routing_id=rid, dma_engine_mask=m),
                   [sm], [], 1000.0, dma="sent", lat=NET)
         sends[0] += 8
-        ts(hb(h, S1), ct, -1, 1, A.mult, A.add)
-        tt(hf(h, SNM), hf(h, NM), hb(h, S1), A.mult)
-        scan(hf(h, AA), ct, hf(h, SNM), A.mult, A.add)
-        ts(hb(h, G2), hb(h, CC), 2, 1, A.mult, A.add)
-        tt(hi(h, AG), hf(h, AA), hb(h, G2), A.mult)
-        if t == 0:
-            ts(hi(h, P1M), hi(h, AG), 2, 4095, A.logical_shift_right, A.bitwise_and)
-        else:
-            ts(hi(h, AG2), hi(h, AG), 2, None, A.logical_shift_right)
-            ts(hi(h, P1), hi(h, AG2), R("AF", t, t + 1), None, A.add)
-            ts(hi(h, P1M), hi(h, P1), 4095, None, A.bitwise_and)
-        ts(hf(h, PP), hi(h, P1M), 4096, 1, A.mult, A.add)
-        mm(pA(h, 3), hf(h, PP), R("IDF", 0, 128))
         for s in range(8):
-            ts(R("MO%d" % h, 128 * s, 128 * s + 128), hb(h, CL), s + 1, None, A.is_equal)
+            ts(mask(h, s), hb(h, CL), s + 1, None, A.is_equal)
         ts(hb(h, E9), hb(h, CL), 9, 100, A.is_lt, A.mult)
-        tt(hb(h, T1), hb(h, CL), hb(h, E9), A.subtract)
-        tt(hb(h, OV), hb(h, T1), R(rm, 0, 128), A.add, waits=[("rm%d%d" % (t, h), 8)], after=[snd])
+        gr = ("ov", t, h)
+        mm(pA(h, 1), R("IDB", 0, 128), hb(h, CL), True, False, gr)
+        mm(pA(h, 1), R("NIB", 0, 128), hb(h, E9), False, False, gr)
+        mm(pA(h, 1), R("IDB", 0, 128), R(rm, 0, 128), False, True, gr, waits=[("rm%d%d" % (t, h), 8)], after=[snd])
+        act(hb(h, OV), pA(h, 1), F.Copy)
         for s in range(8):
             ts(R("MO%d" % h, 1024 + 128 * s, 1152 + 128 * s), hb(h, OV), s + 9, None, A.is_equal)
 
     def middle(t, h):
+        stage[0] = ("middle", t, h)
         gr = ("u", t, h)
         for k in range(16):
             mm(pB(h, 0), R("ZW", 15 - k, 143 - k), R("ZZ", 2048 * h + k, 2048 * h + 2048, 16), k == 0, k == 15, gr)
@@ -357,42 +364,70 @@ def build(g, T, topo, core):
         cp(R("HU%d" % h, 0, 128), hi(h, HH))
         for c in range(4):
             a, b = 2048 * h + 512 * c, 2048 * h + 512 * c + 512
-            tt(R("XD", a, b), (R("X", 0, 4096), R("HU%d" % h, 32 * c, 32 * c + 32)), R("ZZ", a, b), A.subtract)
-            act(R("AE%d" % h, 512 * c, 512 * c + 512), R("XD", a, b), F.Abs)
+            x = (R("X", 0, 4096), R("HU%d" % h, 32 * c, 32 * c + 32))
+            ae = R("AE%d" % h, 512 * c, 512 * c + 512)
+            if c in PLAN["xs"][h]:
+                act(R("XD", a, b), x, F.Copy)
+                pb, gr = R("pb%d" % c, 0, 512), ("xd", t, h, c)
+                mm(pb, R("IDB", 0, 128), R("XD", a, b), True, False, gr)
+                mm(pb, R("NIB", 0, 128), R("ZZ", a, b), False, True, gr)
+                act(ae, pb, F.Abs)
+            else:
+                tt(R("XD", a, b), x, R("ZZ", a, b), A.subtract)
+                act(ae, R("XD", a, b), F.Abs)
+        stage[0] = ("first", t, h)
         ts(hi(h, UI), hi(h, U), 15, None, A.bitwise_and)
-        ts(hb(h, UK), hi(h, UI), K16, None, A.add)
-        tt(R("QB", 128 * h, 128 * h + 128), hb(h, UK), R("MO%d" % h, 0, 128), A.mult)
+        tt(R("QU", 128 * h, 128 * h + 128), hi(h, UI), mask(h, 0), A.mult)
+        ts(R("QE", 128 * h, 128 * h + 128), mask(h, 0), KC_, None, A.mult)
+        stage[0] = ("names", t, h)
+        ct = R("CT%d" % h, 0, 128)
+        act(pB(h, 2), ct, F.Copy, 1.0, -1.0)
+        tt(hf(h, SNM), pB(h, 2), hf(h, NM), A.mult)
+        scan(pB(h, 3), ct, hf(h, SNM), A.mult, A.add)
+        act(hb(h, G2), hb(h, CC), F.Copy, 1.0, 2.0)
+        tt(hi(h, AG), pB(h, 3), hb(h, G2), A.mult)
+        if t == 0:
+            ts(hi(h, P1M), hi(h, AG), 2, 4095, A.logical_shift_right, A.bitwise_and)
+        else:
+            ts(hi(h, AG2), hi(h, AG), 2, None, A.logical_shift_right)
+            ts(hi(h, P1), hi(h, AG2), R("AF", t, t + 1), None, A.add)
+            ts(hi(h, P1M), hi(h, P1), 4095, None, A.bitwise_and)
+        ts(hf(h, PP), hi(h, P1M), 4096, 1, A.mult, A.add)
+        mm(pA(h, 3), hf(h, PP), R("IDF", 0, 128))
 
     def write(t):
-        q = R("pb3", 0, 16)
-        gr = ("q", t)
+        stage[0] = ("write", t, 0)
+        fe, tg = R("pb3", 0, 16), R("pb2", 0, 16)
+        g1, g2 = ("fe", t), ("tg", t)
         for k in range(16):
-            mm(q, R("ZO", 15 - k, 143 - k), R("QB", k, 256, 16), k == 0, k == 15, gr)
-        qi, e, u, em = [R("WI", 16 * c, 16 * c + 16) for c in range(4)]
-        f1, f2 = R("WF", 0, 16), R("WF", 16, 32)
-        ts(qi, q, -1, None, A.add)
-        ts(e, qi, 4, 15, A.logical_shift_right, A.bitwise_and)
-        tt(f1, e, R("BS", 0, 16), A.add)
-        cp(R("FE", 0, 16), f1)
-        act(R("ZF", 0, 256), (R("ZZ", 0, 4096), R("FE", 0, 16)), F.Copy, 0.0, 2.0)
-        ts(u, qi, 15, None, A.bitwise_and)
-        ts(em, qi, 0, 4096, A.is_lt, A.mult)
-        tt(f2, u, R("BS", 0, 16), A.add)
-        f3 = R("WF", 32, 48)
-        tt(f3, f2, em, A.add)
-        cp(R("TG", 0, 16), f3)
+            mm(fe, R("ZO", 15 - k, 143 - k), R("QE", k, 256, 16), k == 0, False, g1)
+        mm(fe, R("IDB", 0, 128), R("BS", 0, 16), False, True, g1)
+        for k in range(16):
+            mm(tg, R("ZO", 15 - k, 143 - k), R("QU", k, 256, 16), k == 0, False, g2)
+            mm(tg, R("ZN", 15 - k, 143 - k), R("M0", k, 256, 16), False, False, g2)
+        mm(tg, R("IDB", 0, 128), R("BS", 0, 16), False, False, g2)
+        mm(tg, R("IDB", 0, 128), R("C4K", 0, 16), False, True, g2)
+        cp(R("FE", 0, 16), fe)
+        cp(R("TG", 0, 16), tg)
+        seg = [1.0 if c % 4 in PLAN["xs"][c // 4] else 2.0 for c in range(8)]
+        c0 = 0
+        for c in range(1, 9):
+            if c == 8 or seg[c] != seg[c0]:
+                act(R("ZF", 32 * c0, 32 * c), (R("ZZ", 0, 4096), R("FE", 2 * c0, 2 * c)), F.Copy, 0.0, seg[c0])
+                c0 = c
         tt(R("SU", 0, 256), (R("XD", 0, 4096), R("FE", 0, 16)), R("ZF", 0, 256), A.add)
         ts(R("SV", 0, 256), R("SU", 0, 256), 1, None, A.arith_shift_right)
         cp((R("X", 0, 8192), R("TG", 0, 16)), R("SV", 0, 256))
         if t < VISITS - 1:
             for h in (0, 1):
-                mm(R("pb2", 0, 128), R("ON", 0, 128), hb(h, EN), h == 0, h == 1, ("a", t))
-            add("V", lambda: g.vector.tensor_reduce(ap(R("AF", 4 + t, 5 + t)), ap(R("pb2", 0, 128)), axis=AxisListType.X, op=A.add), [R("pb2", 0, 128)], [R("AF", 4 + t, 5 + t)], FIX + 128)
+                mm(R("pb1", 0, 128), R("ON", 0, 128), hb(h, EN), h == 0, h == 1, ("a", t))
+            add("V", lambda: g.vector.tensor_reduce(ap(R("AF", 4 + t, 5 + t)), ap(R("pb1", 0, 128)), axis=AxisListType.X, op=A.add), [R("pb1", 0, 128)], [R("AF", 4 + t, 5 + t)], FIX + 128)
             cp(R("AI", 0, 1), R("AF", 4 + t, 5 + t))
             ts(R("AI", 1, 2), R("AI", 0, 1), 255, None, A.bitwise_and)
             cp(R("AF", t + 1, t + 2), R("AI", 1, 2))
 
     def back(t, h):
+        stage[0] = ("back", t, h)
         gr = ("d", t, h)
         for k in range(16):
             mm(pB(h, 3), R("ZO", 15 - k, 143 - k), R("AE%d" % h, k, 2048, 16), k == 0, k == 15, gr)
@@ -405,7 +440,7 @@ def build(g, T, topo, core):
         bank = "pb%d" % (4 + 2 * h)
         for s in (list(range(8, 16)) + list(range(8)) if last else range(16)):
             pr = R("PD%d" % h, 128 * s, 128 * s + 128)
-            tt(pr, pB(h, 2), R("MO%d" % h, 128 * s, 128 * s + 128), A.mult)
+            tt(pr, pB(h, 2), mask(h, s), A.mult)
             o = 64 * (s // 8)
             mm(R(bank, o + s % 8, o + 64, 8), pr, sg)
         sn = "SN%d%d" % (t, h)
@@ -442,6 +477,7 @@ def build(g, T, topo, core):
             if t == 0:
                 start_words(h)
             else:
+                stage[0] = ("join", t, h)
                 q = "%d%d" % (t - 1, h)
                 join(h, R("RO" + q, 0, 64), R("RV" + q, 0, 64), [("rx" + q, 8)], [arr[h]])
                 offsets(h)
@@ -453,10 +489,11 @@ def build(g, T, topo, core):
             arr[h] = back(t, h)
     dma("Q", ("yx", None), R("X", 0, 4096), 6000.0)
     for h in (0, 1):
+        stage[0] = ("join", VISITS, h)
         q = "%d%d" % (VISITS - 1, h)
         join(h, R("SN" + q, 0, 64), R("RV" + q, 0, 64), [("rx" + q, 8)], [arr[h]])
         ts(hf(h, SNM), hi(h, NMI), 1, None, A.add)
-        tt(hf(h, FN), hf(h, SNM), hb(h, LV), A.mult)
+        tt(hf(h, FN), pA(h, 1), hf(h, SNM), A.mult)
         mm(pB(h, 0), hf(h, FN), R("IDF", 0, 128))
         ts(R("YL", 128 * h, 128 * h + 128), pB(h, 0), -1, 0, A.add, A.max)
         ts(hb(h, EL), pB(h, 0), 0.5, None, A.is_gt)
@@ -489,6 +526,9 @@ def schedule(ops):
         for (k, lg) in succ[i]:
             best = max(best, prio[k] + (lg if lg is not None else 0.0))
         prio[i] = best
+    for i in range(n):
+        s = ops[i]["stage"]
+        prio[i] += PLAN["bias"].get((s[0], s[2]), 0.0)
     ready = {e: [] for e in "VSTGQ"}
     at = [0.0] * n
     for i in range(n):

from concourse.bass import DstId, RemoteDMATransfer
from concourse.mybir import dt, AluOpType, AxisListType, ActivationFunctionType

A = AluOpType
F = ActivationFunctionType
VISITS = 4
SCRATCH = {
    "X": ("sbuf", [128, 8192], "bfloat16"),
    "ZZ": ("sbuf", [128, 4096], "bfloat16"), "XD": ("sbuf", [128, 4096], "bfloat16"),
    "QE": ("sbuf", [128, 256], "bfloat16"), "QU": ("sbuf", [128, 256], "bfloat16"), "M0": ("sbuf", [128, 256], "bfloat16"),
    "WL": ("sbuf", [128, 256], "int32"), "WN": ("sbuf", [8, 256], "int32"), "WT": ("sbuf", [128, 1], "int32"), "TH": ("sbuf", [8, 1], "int32"),
    "WLF": ("sbuf", [128, 256], "float32"), "WNB": ("sbuf", [8, 256], "bfloat16"), "THB": ("sbuf", [8, 8], "bfloat16"),
    "CI": ("sbuf", [128, 144], "int32"), "CG": ("sbuf", [128, 144], "int32"), "KI": ("sbuf", [128, 128], "int32"), "CS": ("sbuf", [128, 16], "int32"),
    "PI": ("sbuf", [128, 4], "int32"), "PQ": ("sbuf", [128, 4], "int32"), "PR_": ("sbuf", [128, 4], "int32"),
    "KF": ("sbuf", [128, 16], "float32"),
    "IDB": ("sbuf", [128, 128], "bfloat16"), "NIB": ("sbuf", [128, 128], "bfloat16"), "IDF": ("sbuf", [128, 128], "float32"),
    "BO": ("sbuf", [128, 128], "bfloat16"), "ZO": ("sbuf", [128, 144], "bfloat16"), "ZW": ("sbuf", [128, 144], "bfloat16"),
    "SF": ("sbuf", [128, 8], "bfloat16"), "SGF": ("sbuf", [128, 16], "float32"), "SGB": ("sbuf", [128, 8], "bfloat16"), "SGT": ("sbuf", [8, 128], "bfloat16"),
    "ON": ("sbuf", [128, 128], "bfloat16"), "BIG": ("sbuf", [128, 32], "bfloat16"), "C4K": ("sbuf", [128, 16], "bfloat16"), "ZN": ("sbuf", [128, 144], "bfloat16"), "RS": ("sbuf", [128, 128], "bfloat16"),
    "BS": ("sbuf", [128, 16], "bfloat16"),
    "FE": ("sbuf", [128, 16], "uint16"), "TG": ("sbuf", [128, 16], "uint16"),
    "ZF": ("sbuf", [128, 256], "bfloat16"), "SU": ("sbuf", [128, 256], "int32"), "SV": ("sbuf", [128, 256], "int32"),
    "AI": ("sbuf", [128, 8], "int32"), "AF": ("sbuf", [128, 8], "float32"),
    "YL": ("sbuf", [128, 256], "float32"), "YN": ("sbuf", [8, 256], "float32"),
}
for _h in (0, 1):
    SCRATCH["V%d" % _h] = ("sbuf", [128, 2064], "bfloat16")
    for _n in ("AD", "MK", "AE", "MO"):
        SCRATCH["%s%d" % (_n, _h)] = ("sbuf", [128, 2048], "bfloat16")
    SCRATCH["PD%d" % _h] = ("sbuf", [128, 2048], "float32")
    SCRATCH["OF%d" % _h] = ("sbuf", [128, 128], "uint16")
    SCRATCH["HU%d" % _h] = ("sbuf", [128, 128], "uint16")
    SCRATCH["CT%d" % _h] = ("sbuf", [128, 144], "bfloat16")
    SCRATCH["HB%d" % _h] = ("sbuf", [128, 128 * 16], "bfloat16")
    SCRATCH["HF%d" % _h] = ("sbuf", [128, 128 * 6], "float32")
    SCRATCH["HI%d" % _h] = ("sbuf", [128, 128 * 12], "int32")
for _t in range(VISITS):
    for _h in (0, 1):
        SCRATCH["SN%d%d" % (_t, _h)] = ("sbuf", [128, 128], "float32")
        SCRATCH["SM%d%d" % (_t, _h)] = ("sbuf", [128, 128], "bfloat16")
        SCRATCH["RO%d%d" % (_t, _h)] = ("sbuf", [128, 64], "float32")
        SCRATCH["RV%d%d" % (_t, _h)] = ("sbuf", [128, 64], "float32")
        SCRATCH["RM%d%d" % (_t, _h)] = ("sbuf", [128, 128], "bfloat16")
for _b in range(8):
    SCRATCH["pb%d" % _b] = ("psum", [128, 512], "float32")
ENGS = "VSTG"
SEMAPHORES = ["e" + e for e in ENGS] + ["sent"] + ["rx%d%d" % (t, h) for t in range(VISITS) for h in (0, 1)] \
    + ["rm%d%d" % (t, h) for t in range(VISITS) for h in (0, 1)] + ["dm%d" % i for i in range(12)]

CYC, FIX, GAT, SCA, PE, HOP, OWN, NET = 1.0, 30.0, 1.6, 4.0, 0.5, 110.0, 40.0, 2800.0


def R(b, c0, c1, step=1, p=128):
    return (b, c0, c1, step, p)


def _n(r):
    return (r[2] - r[1] + r[3] - 1) // r[3]


def _over(a, b):
    if a[2] <= b[1] or b[2] <= a[1]:
        return False
    if a[3] == b[3] and a[3] > 1 and (a[1] - b[1]) % a[3]:
        return False
    return True


def _wide(b):
    return 4 if SCRATCH[b][2] in ("float32", "int32") else 2


PLAN = {"gv": {0: (), 1: (0, 1, 2, 3)}, "xs": {0: (), 1: (2, 3)}, "bias": {}}


def build(g, T, topo, core):
    ops = []
    hist = {}
    banks = {}
    ndma = [0]
    stage = [("load", 0, 0)]
    blast = {}

    def ap(r):
        if r is None or isinstance(r, (int, float)):
            return r
        if len(r) == 2:
            w, o = r
            if o is None:
                return T[w][:]
            return ap(w).indirect(ap(o))
        b, c0, c1, st, p = r
        full = SCRATCH[b][1][1]
        if st == 1:
            return T[b][0:p, c0:c1]
        return T[b][0:p, c0:min(c1, full):st]

    def regs(r):
        if r is None or isinstance(r, (int, float)):
            return []
        if len(r) == 2:
            return [] if r[1] is None else [r[0], r[1]]
        return [r]

    def add(eng, fn, reads, writes, cost, grp=None, dma=False, waits=(), after=(), lat=None):
        i = len(ops)
        deps = {}

        def dep(j, hard):
            if j != i:
                deps[j] = deps.get(j, False) or hard
        for r in reads:
            for (q, j, w) in hist.get(r[0], ()):
                if w and _over(q, r) and not (grp is not None and ops[j]["grp"] == grp):
                    dep(j, True)
        for r in writes:
            for (q, j, w) in hist.get(r[0], ()):
                if _over(q, r) and not (grp is not None and ops[j]["grp"] == grp):
                    dep(j, w or ops[j]["eng"] != eng or ops[j]["dma"])
        for b in set(r[0] for r in list(reads) + list(writes) if r[0][:2] == "pb"):
            ph = banks.setdefault(b, [None, [], []])
            if ph[0] != eng:
                ph[2] = ph[1]
                ph[0], ph[1] = eng, []
            ph[1].append(i)
            for j in ph[2]:
                dep(j, True)
        if eng == "T":
            for b in set(r[0] for r in writes):
                if b in blast and ops[blast[b]]["grp"] != grp:
                    dep(blast[b], False)
                blast[b] = i
        if grp is not None:
            for j in range(i - 1, -1, -1):
                if ops[j]["grp"] == grp:
                    dep(j, False)
                    break
        for j in after:
            dep(j, False)
        for r in writes:
            lst = hist.setdefault(r[0], [])
            if r[3] == 1:
                lst[:] = [e for e in lst if not (e[0][1] >= r[1] and e[0][2] <= r[2] and e[0][4] <= r[4])]
            lst.append((r, i, True))
        for r in reads:
            hist.setdefault(r[0], []).append((r, i, False))
        ops.append({"stage": stage[0], "eng": eng, "fn": fn, "deps": deps, "cost": cost, "grp": grp, "dma": dma, "waits": waits, "lat": lat, "after": after})
        return i

    def vcost(out, ins, two=False):
        n = _n(out)
        w = max(_wide(r[0]) for q in [out] + list(ins) for r in regs(q)[:1])
        ps = any(r[0][:2] == "pb" for q in ins for r in regs(q))
        f = (1 if ps else 2) if two else (0.5 if w == 2 and not ps and out[0][:2] != "pb" else 1)
        for q in ins:
            if not isinstance(q, (int, float)) and q is not None and len(q) == 2:
                f = max(f if two is False else 1, GAT)
        return FIX + CYC * max(64, n * f)

    def tt(out, a, b, op, **kw):
        return add("V", lambda: g.vector.tensor_tensor(ap(out), ap(a), ap(b), op), regs(a) + regs(b), regs(out), vcost(out, [a, b], True), **kw)

    def ts(out, a, s1, s2, op0, op1=None, **kw):
        if op1 is None:
            fn = lambda: g.vector.tensor_scalar(ap(out), ap(a), ap(s1), None, op0)
        else:
            fn = lambda: g.vector.tensor_scalar(ap(out), ap(a), ap(s1), ap(s2), op0, op1)
        return add("V", fn, regs(a) + regs(s1) + regs(s2), regs(out), vcost(out, [a]), **kw)

    def cp(out, a, **kw):
        if len(out) == 2:
            return add("V", lambda: g.vector.tensor_copy(ap(out), ap(a)), regs(a) + [out[1]], [out[0]], FIX + CYC * SCA * _n(a), **kw)
        return add("V", lambda: g.vector.tensor_copy(ap(out), ap(a)), regs(a), regs(out), vcost(out, [a]), **kw)

    def scan(out, d0, d1, op0, op1):
        return add("V", lambda: g.vector.tensor_tensor_scan(ap(out), ap(d0), ap(d1), 0.0, op0, op1), regs(d0) + regs(d1), regs(out), vcost(out, [d0, d1]))

    def ms(out, val):
        return add("V", lambda: g.vector.memset(ap(out), val), [], regs(out), vcost(out, []))

    def act(out, a, func, bias=0.0, scale=1.0):
        n = _n(out) * (GAT if len(a) == 2 else 1)
        return add("S", lambda: g.scalar.activation(ap(out), ap(a), func, bias=ap(bias), scale=scale), regs(a) + regs(bias), regs(out), FIX + 20 + CYC * max(64, n))

    def mm(out, lhsT, rhs, start=True, stop=True, grp=None, **kw):
        f = 4 if SCRATCH[lhsT[0]][2] == "float32" else 1
        return add("T", lambda: g.tensor.matmul(ap(out), ap(lhsT), ap(rhs), start, stop), regs(lhsT) + regs(rhs), regs(out), 8 + PE * f * max(64, _n(rhs)), grp=grp, **kw)

    def dma(q, out, a, cost=2500.0):
        i = ndma[0]
        ndma[0] += 1
        eng = g.sync if q == "Q" else g.scalar
        return add(q, lambda: eng.dma_start(ap(out), ap(a)), regs(a), regs(out), 100.0, dma="dm%d" % i, lat=cost)

    def io(name, c0=None, c1=None):
        return (name, None)

    dma("Q", R("WL", 0, 256), ("wl", None))
    dma("Q", R("X", 0, 4096), ("xv", None), 6000.0)
    dma("S", R("TH", 0, 1, 1, 8), ("th", None))
    dma("S", R("WN", 0, 256, 1, 8), ("wn", None))
    dma("S", R("WT", 0, 1), ("wt", None))
    add("G", lambda: g.iota(ap(R("CI", 0, 144)), [[1, 144]], 0, 0), [], [R("CI", 0, 144)], 400.0)
    add("G", lambda: g.iota(ap(R("PI", 0, 1)), [[1, 1]], 0, 1), [], [R("PI", 0, 1)], 150.0)
    PI = R("PI", 0, 1)
    PF, PG, T15, KC_, L16, WC, TB, PL = [R("KF", c, c + 1) for c in range(8)]
    C128 = R("CI", 0, 128)
    for h in (0, 1):
        ms(R("V%d" % h, 0, 16), 0.0)
        ms(R("CT%d" % h, 128, 144), 0.0)
    ms(R("BIG", 0, 32), 512.0)
    ms(R("C4K", 0, 16), 4096.0)
    ms(R("ON", 0, 128), 1.0)
    cp(PF, PI)
    ts(R("PQ", 0, 1), PI, 4, None, A.logical_shift_right)
    ts(R("PR_", 0, 1), PI, 15, None, A.bitwise_and)
    cp(PG, R("PQ", 0, 1))
    ts(T15, R("PQ", 0, 1), 16, 15, A.mult, A.add)
    cp(KC_, R("PR_", 0, 1))
    ts(L16, R("PR_", 0, 1), 16, None, A.mult)
    ts(R("CG", 0, 144), R("CI", 0, 144), 4, None, A.logical_shift_right)
    ts(R("SGT", 0, 128, 1, 8), R("CG", 0, 128, 1, 8), R("KF", 0, 1, 1, 8), None, A.is_equal)
    ts(R("IDB", 0, 128), C128, PF, None, A.is_equal)
    ts(R("NIB", 0, 128), C128, PF, -1, A.is_equal, A.mult)
    ts(R("IDF", 0, 128), C128, PF, None, A.is_equal)
    ts(R("BO", 0, 128), R("CG", 0, 128), PG, None, A.is_equal)
    ts(R("ZO", 0, 144), R("CI", 0, 144), T15, None, A.is_equal)
    ts(R("ZN", 0, 144), R("CI", 0, 144), T15, -4096, A.is_equal, A.mult)
    ts(R("SF", 0, 8), R("CI", 0, 8), 16, PF, A.mult, A.is_equal)
    ts(R("CS", 0, 16), R("CI", 0, 16), 7, None, A.bitwise_and)
    ts(R("SGF", 0, 16), R("CS", 0, 16), PG, None, A.is_equal)
    ts(R("SGB", 0, 8), R("CI", 0, 8), PG, None, A.is_equal)
    ts(R("KI", 0, 128), C128, 15, None, A.bitwise_and)
    ts(R("RS", 0, 128), R("KI", 0, 128), 0, None, A.is_gt)
    ts(R("BS", 0, 16), R("CI", 0, 16), 256, L16, A.mult, A.add)
    cp(R("THB", 0, 1, 1, 8), R("TH", 0, 1, 1, 8))
    cp(R("WNB", 0, 256, 1, 8), R("WN", 0, 256, 1, 8))
    cp(WC, R("WT", 0, 1))
    ts(R("ZW", 0, 144), R("CI", 0, 144), T15, WC, A.is_equal, A.mult)
    mm(R("pb3", 0, 1), R("SGT", 0, 128, 1, 8), R("THB", 0, 1, 1, 8))
    ts(TB, R("pb3", 0, 1), 0.5, None, A.add)

    def H(kind, h, s, c0=0, c1=128, step=1):
        return R("%s%d" % (kind, h), 128 * s + c0, 128 * s + c1, step)

    def hb(h, s, *a):
        return H("HB", h, s, *a)

    def hf(h, s, *a):
        return H("HF", h, s, *a)

    def hi(h, s, *a):
        return H("HI", h, s, *a)
    NL_, LV, EN, CU, CC, S1, G2, CD, CL, EL, E9, T1, OV, GL, UK = range(15)
    NM, SNM, AA, PP, KC, FN = range(6)
    JI, NMI, AG, AG2, P1, P1M, UI, U, Y, HH, Q2, Q3 = range(12)

    def pA(h, r):
        return R("pb%d" % (4 + 2 * h), 128 * r, 128 * r + 128)

    def pB(h, r):
        return R("pb%d" % (5 + 2 * h), 128 * r, 128 * r + 128)
    rank = T.rank_of(core)
    sends = [0]

    def addr(d):
        dst = T.cores[(rank + d) % 4]
        rid, pid, _s = topo.addr(dst)
        return dst, rid, pid

    def start_words(h):
        w = R("WL", 128 * h, 128 * h + 128)
        cp(R("OF%d" % h, 0, 128), w)
        cp(R("WLF", 128 * h, 128 * h + 128), w)
        mm(pA(h, 0), R("WLF", 128 * h, 128 * h + 128), R("IDF", 0, 128))
        act(hf(h, NM), pA(h, 0), F.Copy)
        mm(pB(h, 0), R("WNB", 128 * h, 128 * h + 128, 1, 8), R("SGT", 0, 128, 1, 8))
        tt(pA(h, 1), pB(h, 0), R("KI", 0, 128), A.is_gt)
        ts(hb(h, NL_), pA(h, 1), -1, 1, A.mult, A.add)

    def join(h, own, ov, waits, after):
        tt(hi(h, JI, 0, 64), own, ov, A.add, waits=waits, after=after)
        ts(hi(h, NMI, 0, 128, 2), hi(h, JI, 0, 64), 12, 4095, A.logical_shift_right, A.bitwise_and)
        ts(hi(h, NMI, 1, 128, 2), hi(h, JI, 0, 64), 4095, None, A.bitwise_and)
        cp(hf(h, NM), hi(h, NMI))
        ts(hb(h, NL_, 0, 128, 2), hi(h, JI, 0, 64), 0, None, A.is_lt)
        ts(hb(h, NL_, 1, 128, 2), hi(h, JI, 0, 64), 0, None, A.is_lt)
        act(pA(h, 1), hb(h, NL_), F.Copy, 1.0, -1.0)

    def offsets(h):
        mm(pB(h, 0), hf(h, NM), R("IDF", 0, 128))
        cp(R("OF%d" % h, 0, 128), pB(h, 0))

    def mask(h, s):
        return R("M0", 128 * h, 128 * h + 128) if s == 0 else R("MO%d" % h, 128 * s, 128 * s + 128)

    def front(t, h):
        stage[0] = ("front", t, h)
        v, ad, mk = "V%d" % h, "AD%d" % h, "MK%d" % h
        for c in range(4):
            o, i = R(v, 16 + 512 * c, 528 + 512 * c), (R("X", 0, 4096), R("OF%d" % h, 32 * c, 32 * c + 32))
            if c in PLAN["gv"][h]:
                cp(o, i)
            else:
                act(o, i, F.Copy)
        for c in range(4):
            b = R("pb%d" % c, 0, 512)
            gr = ("df", t, h, c)
            mm(b, R("IDB", 0, 128), R(v, 16 + 512 * c, 528 + 512 * c), True, False, gr)
            mm(b, R("NIB", 0, 128), R(v, 15 + 512 * c, 527 + 512 * c), False, False, gr)
            mm(R("pb%d" % c, 0, 512, 16), R("IDB", 0, 128), R("BIG", 0, 32), False, True, gr)
            act(R(ad, 512 * c, 512 * c + 512), b, F.Abs)
            mm(b, R("BO", 0, 128), R(ad, 512 * c, 512 * c + 512))
            act(R(mk, 512 * c, 512 * c + 512), b, F.Sign, TB, -1.0)
            scan(R("ZZ", 2048 * h + 512 * c, 2048 * h + 512 * c + 512), R(mk, 512 * c, 512 * c + 512), R(v, 16 + 512 * c, 528 + 512 * c), A.mult, A.max)
        for k in range(16):
            mm(R("pb%d" % (4 + 2 * h), k, 128, 16), R(mk, k, 2048, 16), R("SF", 0, 8))
        ct = R("CT%d" % h, 0, 128)
        tt(ct, pA(h, 0), hb(h, NL_), A.is_gt)
        tt(hb(h, EN), pA(h, 1), R("CT%d" % h, 1, 129), A.subtract)
        scan(pA(h, 0), R("RS", 0, 128), hb(h, EN), A.mult, A.add)
        scan(hb(h, CC), ct, R("ON", 0, 128), A.mult, A.add)
        tt(hb(h, CD), pA(h, 0), hb(h, EN), A.mult)
        mm(pA(h, 1), hb(h, CC), R("IDB", 0, 128))
        mm(pA(h, 2), hb(h, CD), R("IDB", 0, 128))
        act(hf(h, KC), pA(h, 1), F.Copy, 0.0, 19552.0)
        act(hb(h, GL), pA(h, 1), F.Copy, 1.0, 2.0)
        act(hb(h, CL), pA(h, 2), F.Copy)
        act(hb(h, EL), hb(h, CL), F.Sign)
        mm(pA(h, 0), R("BO", 0, 128), hb(h, EL))
        sm = R("SM%d%d" % (t, h), 0, 128)
        act(sm, pA(h, 0), F.Copy)
        dst, rid, pid = addr(-1)
        es = topo.engines(core, dst)
        m = 0
        for e in es[:8]:
            m |= 1 << e
        rm = "RM%d%d" % (t, h)
        snd = add("G", lambda: g.remote_dma(out_ap=T[rm][:], in_ap=ap(sm), remote_sem=T.sem["rm%d%d" % (t, h)], local_sem=T.sem["sent"], pid=pid, routing_id=rid, dma_engine_mask=m),
                  [sm], [], 1000.0, dma="sent", lat=NET)
        sends[0] += 8
        for s in range(8):
            ts(mask(h, s), hb(h, CL), s + 1, None, A.is_equal)
        ts(hb(h, E9), hb(h, CL), 9, 100, A.is_lt, A.mult)
        gr = ("ov", t, h)
        mm(pA(h, 1), R("IDB", 0, 128), hb(h, CL), True, False, gr)
        mm(pA(h, 1), R("NIB", 0, 128), hb(h, E9), False, False, gr)
        mm(pA(h, 1), R("IDB", 0, 128), R(rm, 0, 128), False, True, gr, waits=[("rm%d%d" % (t, h), 8)], after=[snd])
        act(hb(h, OV), pA(h, 1), F.Copy)
        for s in range(8):
            ts(R("MO%d" % h, 1024 + 128 * s, 1152 + 128 * s), hb(h, OV), s + 9, None, A.is_equal)

    def middle(t, h):
        stage[0] = ("middle", t, h)
        gr = ("u", t, h)
        for k in range(16):
            mm(pB(h, 0), R("ZW", 15 - k, 143 - k), R("ZZ", 2048 * h + k, 2048 * h + 2048, 16), k == 0, k == 15, gr)
        cp(hi(h, UI), pB(h, 0))
        ts(hi(h, U), hi(h, UI), 4095, None, A.bitwise_and)
        ts(pB(h, 1), hi(h, U), 1184, None, A.add)
        tt(pB(h, 2), pB(h, 1), hi(h, U), A.mult)
        tt(hi(h, Y), pB(h, 2), hf(h, KC), A.add)
        ts(hi(h, HH), hi(h, Y), 5, 4095, A.logical_shift_right, A.bitwise_and)
        cp(R("HU%d" % h, 0, 128), hi(h, HH))
        for c in range(4):
            a, b = 2048 * h + 512 * c, 2048 * h + 512 * c + 512
            x = (R("X", 0, 4096), R("HU%d" % h, 32 * c, 32 * c + 32))
            ae = R("AE%d" % h, 512 * c, 512 * c + 512)
            if c in PLAN["xs"][h]:
                act(R("XD", a, b), x, F.Copy)
                pb, gr = R("pb%d" % c, 0, 512), ("xd", t, h, c)
                mm(pb, R("IDB", 0, 128), R("XD", a, b), True, False, gr)
                mm(pb, R("NIB", 0, 128), R("ZZ", a, b), False, True, gr)
                act(ae, pb, F.Abs)
            else:
                tt(R("XD", a, b), x, R("ZZ", a, b), A.subtract)
                act(ae, R("XD", a, b), F.Abs)
        stage[0] = ("first", t, h)
        ts(hi(h, UI), hi(h, U), 15, None, A.bitwise_and)
        tt(R("QU", 128 * h, 128 * h + 128), hi(h, UI), mask(h, 0), A.mult)
        ts(R("QE", 128 * h, 128 * h + 128), mask(h, 0), KC_, None, A.mult)
        stage[0] = ("names", t, h)
        ct = R("CT%d" % h, 0, 128)
        act(pB(h, 2), ct, F.Copy, 1.0, -1.0)
        tt(hf(h, SNM), pB(h, 2), hf(h, NM), A.mult)
        scan(pB(h, 3), ct, hf(h, SNM), A.mult, A.add)
        act(hb(h, G2), hb(h, CC), F.Copy, 1.0, 2.0)
        tt(hi(h, AG), pB(h, 3), hb(h, G2), A.mult)
        if t == 0:
            ts(hi(h, P1M), hi(h, AG), 2, 4095, A.logical_shift_right, A.bitwise_and)
        else:
            ts(hi(h, AG2), hi(h, AG), 2, None, A.logical_shift_right)
            ts(hi(h, P1), hi(h, AG2), R("AF", t, t + 1), None, A.add)
            ts(hi(h, P1M), hi(h, P1), 4095, None, A.bitwise_and)
        ts(hf(h, PP), hi(h, P1M), 4096, 1, A.mult, A.add)
        mm(pA(h, 3), hf(h, PP), R("IDF", 0, 128))

    def write(t):
        stage[0] = ("write", t, 0)
        fe, tg = R("pb3", 0, 16), R("pb2", 0, 16)
        g1, g2 = ("fe", t), ("tg", t)
        for k in range(16):
            mm(fe, R("ZO", 15 - k, 143 - k), R("QE", k, 256, 16), k == 0, False, g1)
        mm(fe, R("IDB", 0, 128), R("BS", 0, 16), False, True, g1)
        for k in range(16):
            mm(tg, R("ZO", 15 - k, 143 - k), R("QU", k, 256, 16), k == 0, False, g2)
            mm(tg, R("ZN", 15 - k, 143 - k), R("M0", k, 256, 16), False, False, g2)
        mm(tg, R("IDB", 0, 128), R("BS", 0, 16), False, False, g2)
        mm(tg, R("IDB", 0, 128), R("C4K", 0, 16), False, True, g2)
        cp(R("FE", 0, 16), fe)
        cp(R("TG", 0, 16), tg)
        seg = [1.0 if c % 4 in PLAN["xs"][c // 4] else 2.0 for c in range(8)]
        c0 = 0
        for c in range(1, 9):
            if c == 8 or seg[c] != seg[c0]:
                act(R("ZF", 32 * c0, 32 * c), (R("ZZ", 0, 4096), R("FE", 2 * c0, 2 * c)), F.Copy, 0.0, seg[c0])
                c0 = c
        tt(R("SU", 0, 256), (R("XD", 0, 4096), R("FE", 0, 16)), R("ZF", 0, 256), A.add)
        ts(R("SV", 0, 256), R("SU", 0, 256), 1, None, A.arith_shift_right)
        cp((R("X", 0, 8192), R("TG", 0, 16)), R("SV", 0, 256))
        if t < VISITS - 1:
            for h in (0, 1):
                mm(R("pb1", 0, 128), R("ON", 0, 128), hb(h, EN), h == 0, h == 1, ("a", t))
            add("V", lambda: g.vector.tensor_reduce(ap(R("AF", 4 + t, 5 + t)), ap(R("pb1", 0, 128)), axis=AxisListType.X, op=A.add), [R("pb1", 0, 128)], [R("AF", 4 + t, 5 + t)], FIX + 128)
            cp(R("AI", 0, 1), R("AF", 4 + t, 5 + t))
            ts(R("AI", 1, 2), R("AI", 0, 1), 255, None, A.bitwise_and)
            cp(R("AF", t + 1, t + 2), R("AI", 1, 2))

    def back(t, h):
        stage[0] = ("back", t, h)
        gr = ("d", t, h)
        for k in range(16):
            mm(pB(h, 3), R("ZO", 15 - k, 143 - k), R("AE%d" % h, k, 2048, 16), k == 0, k == 15, gr)
        tt(pB(h, 1), pB(h, 3), hb(h, GL), A.mult)
        tt(hi(h, Q2), pB(h, 1), hi(h, HH), A.add)
        ts(hi(h, Q3), hi(h, Q2), 4095, None, A.bitwise_and)
        tt(pB(h, 2), pA(h, 3), hi(h, Q3), A.add)
        last = t == VISITS - 1
        sg = R("SGF", 0, 8) if last else R("SGF", 7, 15)
        bank = "pb%d" % (4 + 2 * h)
        for s in (list(range(8, 16)) + list(range(8)) if last else range(16)):
            pr = R("PD%d" % h, 128 * s, 128 * s + 128)
            tt(pr, pB(h, 2), mask(h, s), A.mult)
            o = 64 * (s // 8)
            mm(R(bank, o + s % 8, o + 64, 8), pr, sg)
        sn = "SN%d%d" % (t, h)
        act(R(sn, 0, 64), R(bank, 0, 64), F.Copy, -1.0)
        act(R(sn, 64, 128), R(bank, 64, 128), F.Copy)
        ro, rv, rx = "RO%d%d" % (t, h), "RV%d%d" % (t, h), "rx%d%d" % (t, h)
        d1, r1, p1 = addr(1)
        d2, r2, p2 = addr(2)
        e1, e2 = topo.engines(core, d1), topo.engines(core, d2)
        if last:
            m = 0
            for e in e1[:8]:
                m |= 1 << e
            sends[0] += 8
            return add("G", lambda: g.remote_dma(out_ap=T[rv][:], in_ap=ap(R(sn, 64, 128)), remote_sem=T.sem[rx], local_sem=T.sem["sent"], pid=p1, routing_id=r1, dma_engine_mask=m),
                       [R(sn, 64, 128)], [], 1000.0, dma="sent", lat=NET)
        m1 = m2 = 0
        for e in e1[:4]:
            m1 |= 1 << e
        for e in [e for e in e2 if e not in e1[:4]][:4]:
            m2 |= 1 << e
        sends[0] += 8

        def fused():
            return g.remote_dma_fused([
                RemoteDMATransfer(dst_ids=[DstId(rid=r1, pnc=p1)], dma_engine_mask=m1, remote_sem=T.sem[rx], src=ap(R(sn, 0, 64)), dst=T[ro][:]),
                RemoteDMATransfer(dst_ids=[DstId(rid=r2, pnc=p2)], dma_engine_mask=m2, remote_sem=T.sem[rx], src=ap(R(sn, 64, 128)), dst=T[rv][:]),
            ], local_sem=T.sem["sent"])
        return add("G", fused, [R(sn, 0, 128)], [], 1200.0, dma="sent", lat=NET)

    arr = {}
    for t in range(VISITS):
        for h in (0, 1):
            if t == 0:
                start_words(h)
            else:
                stage[0] = ("join", t, h)
                q = "%d%d" % (t - 1, h)
                join(h, R("RO" + q, 0, 64), R("RV" + q, 0, 64), [("rx" + q, 8)], [arr[h]])
                offsets(h)
        for h in (0, 1):
            front(t, h)
            middle(t, h)
        write(t)
        for h in (0, 1):
            arr[h] = back(t, h)
    dma("Q", ("yx", None), R("X", 0, 4096), 6000.0)
    for h in (0, 1):
        stage[0] = ("join", VISITS, h)
        q = "%d%d" % (VISITS - 1, h)
        join(h, R("SN" + q, 0, 64), R("RV" + q, 0, 64), [("rx" + q, 8)], [arr[h]])
        ts(hf(h, SNM), hi(h, NMI), 1, None, A.add)
        tt(hf(h, FN), pA(h, 1), hf(h, SNM), A.mult)
        mm(pB(h, 0), hf(h, FN), R("IDF", 0, 128))
        ts(R("YL", 128 * h, 128 * h + 128), pB(h, 0), -1, 0, A.add, A.max)
        ts(hb(h, EL), pB(h, 0), 0.5, None, A.is_gt)
        mm(R("pb%d" % (4 + 2 * h), 0, 128, 1, 8), R("SGB", 0, 8), hb(h, EL))
        act(R("YN", 128 * h, 128 * h + 128, 1, 8), R("pb%d" % (4 + 2 * h), 0, 128, 1, 8), F.Copy)
    dma("Q", ("yl", None), R("YL", 0, 256))
    dma("Q", ("yn", None), R("YN", 0, 256, 1, 8))
    return ops, sends[0]


def schedule(ops):
    n = len(ops)
    succ = [[] for _ in range(n)]
    npred = [0] * n

    def lag(j, i, hard):
        a, b = ops[j], ops[i]
        if not hard and j not in b["after"]:
            return None
        if a["lat"] is not None:
            return a["cost"] + a["lat"]
        return a["cost"] + (OWN if a["eng"] == b["eng"] else HOP)
    for i in range(n):
        for j, hard in ops[i]["deps"].items():
            succ[j].append((i, lag(j, i, hard)))
            npred[i] += 1
    prio = [0.0] * n
    for i in range(n - 1, -1, -1):
        best = ops[i]["cost"]
        for (k, lg) in succ[i]:
            best = max(best, prio[k] + (lg if lg is not None else 0.0))
        prio[i] = best
    for i in range(n):
        s = ops[i]["stage"]
        prio[i] += PLAN["bias"].get((s[0], s[2]), 0.0)
    ready = {e: [] for e in "VSTGQ"}
    at = [0.0] * n
    for i in range(n):
        if npred[i] == 0:
            ready[ops[i]["eng"]].append(i)
    free = {e: 0.0 for e in ready}
    order = []
    start = [0.0] * n
    while len(order) < n:
        best = None
        for e in ready:
            if not ready[e]:
                continue
            t0 = min(max(free[e], at[i]) for i in ready[e])
            if best is None or t0 < best[0]:
                best = (t0, e)
        t0, e = best
        i = max((k for k in ready[e] if max(free[e], at[k]) <= t0 + 1e-9), key=lambda k: (prio[k], -k))
        ready[e].remove(i)
        start[i] = t0
        order.append(i)
        free[e] = t0 + ops[i]["cost"]
        for (k, lg) in succ[i]:
            at[k] = max(at[k], t0 + (lg if lg is not None else 0.0))
            npred[k] -= 1
            if npred[k] == 0:
                ready[ops[k]["eng"]].append(k)
    return order, start, free


def rank_program(g, core, T, topo):
    if T.rank_of(core) is None:
        return
    ops, nsent = build(g, T, topo, core)
    order, start, free = schedule(ops)
    queue = {"V": g.vector, "S": g.scalar, "T": g.tensor, "G": g, "Q": g.sync}
    need = set()
    for i in order:
        for j, hard in ops[i]["deps"].items():
            if hard and not ops[j]["dma"]:
                need.add(j)
    count = {e: 0 for e in queue}
    mark = {}
    know = {e: {} for e in queue}
    snap = {}
    for i in order:
        o = ops[i]
        e = o["eng"]
        want = {}
        for j, hard in o["deps"].items():
            if not hard or ops[j]["dma"] == "sent":
                continue
            s, v = mark[j]
            if know[e].get(s, 0) < v:
                want.setdefault(s, []).append((v, j))
        todo = sorted(((max(l)[0], s, max(l)[1]) for s, l in want.items()), key=lambda x: -start[x[2]])
        for v, s, j in todo:
            if know[e].get(s, 0) >= v:
                continue
            queue[e].wait_ge(T.sem[s], v)
            know[e][s] = v
            for s2, v2 in snap[j].items():
                if know[e].get(s2, 0) < v2:
                    know[e][s2] = v2
        for (s, v) in o["waits"]:
            queue[e].wait_ge(T.sem[s], v)
        ins = o["fn"]()
        snap[i] = dict(know[e])
        if o["dma"] and o["dma"] != "sent":
            ins.then_inc(T.sem[o["dma"]], 16)
            mark[i] = (o["dma"], 16)
        elif i in need:
            count[e] += 1
            ins.then_inc(T.sem["e" + e], 1)
            mark[i] = ("e" + e, count[e])
    for e in ENGS:
        if count[e]:
            g.wait_ge(T.sem["e" + e], count[e])
    g.wait_ge(T.sem["sent"], nsent)
    for o in ops:
        if o["dma"] and o["dma"] != "sent":
            g.wait_ge(T.sem[o["dma"]], 16)
